import numpy as np, ml_dtypes
CORES = [40,41,42,43,44,45,46,47]
N = 8
BF = ml_dtypes.bfloat16
W, C, RO, SH = 8192, 256, 4, 5
def parts(rng):
    cov = np.where(rng.random((N, 8, 1, W)) < 0.15, 0, rng.integers(0, 256, (N, 8, 16, W)))
    share = rng.choice(np.array([0.0, 0.1, 0.2, 0.3, 0.5, 0.8]), (N, 8, 1, C))
    tst = np.where(rng.random((N, 8, 16, C)) < share, 256, rng.integers(0, 256, (N, 8, 16, C)))
    return cov, tst, rng.integers(0, 160, (N, 8, 16, C)), rng.integers(200, 2000, (N, 8))
def pack(cov, tst, pr, th):
    return {"cov": np.ascontiguousarray(cov.reshape(N, 128, W)).astype(np.float32).astype(BF), "tst": np.ascontiguousarray(tst.reshape(N, 128, C)).astype(np.int32),
            "pr": np.ascontiguousarray(pr.reshape(N, 128, C)).astype(np.float32).astype(BF), "th": np.ascontiguousarray(th.reshape(N, 8, 1)).astype(np.int32)}
def setup_inputs(rng):
    return pack(*parts(rng))
def setup_inputs_corners(rng):
    cov, tst, pr, th = parts(rng)
    c = np.arange(C); lane = np.arange(16)[:, None]; full = rng.integers(0, 256, (N, 8, 16, C))
    th = rng.choice(np.array([0, 1, 500, 4080]), (N, 8))
    for r in range(N):
        for g in range(8):
            k = (g + r) % 8; x = full[r, g]
            if k == 1: x = np.full((16, C), 256)
            elif k == 2: x = np.where(lane == c % 16, 256, x)
            elif k == 3: x = np.where((lane + c) % 2 == 1, 256, x)
            elif k == 4:
                x = np.repeat(x[:, :1], C, axis=1); pr[r, g] = np.repeat(pr[r, g][:, :1], C, axis=1); th[r, g] = 0
            elif k == 5: x = np.where((lane == c % 16) | (lane == (c + 1) % 16), x, 256)
            elif k == 6:
                cov[r, g][:, rng.random(W) < 0.7] = 0; th[r, g] = 0
            elif k == 7: pr[r, g] = 255 * rng.integers(0, 2, (1, C))
            tst[r, g] = x
    q = rng.permutation(N); th[q[0]] = 0; th[q[1]] = 4080
    r = int(q[0]); g = (8 - r) % 8
    cov[r, g, 0] = 0; cov[r, g, 1:] = rng.integers(1, 256, (15, W))
    pr[r, g, :, 0::2] = 255; pr[r, g, :, 1::2] = 0
    k = np.arange(C // 2); p = 1 + k % 14; v = rng.integers(0, 256, (2, C // 2)); x = np.full((16, C), 256)
    for odd in range(2):
        x[p, 2 * k + odd] = v[0]; x[p + 1, 2 * k + odd] = v[1]
    tst[r, g] = x
    return pack(cov, tst, pr, th)
def pairs(rng, low):
    x = rng.integers(0, 256, 2 ** 15); y = rng.integers(0, 256, 2 ** 15); i = rng.integers(0, 16, 2 ** 15)
    col, at = np.unique(((((2 * x + 1) * (2 * y + 1)) >> 4) + 613 * i) & (W - 1), return_index=True)
    at = rng.permutation(at[col >= low])
    return x[at], y[at], i[at]
def lone(rng, x, y, i):
    k = len(x); c = np.arange(k); v = np.full((16, k), 256)
    v[i, c] = x; v[(i + 1) & 15, c] = y
    for d in range(3, 15, 2): v[(i + d) & 15, c] = rng.integers(0, 256, k)
    return v
def setup_inputs_crowd(rng):
    cov, tst, pr, th = parts(rng)
    a = int(rng.integers(0, N)); b = (a + 1) % N; d = (a + 2) % N
    v = rng.integers(0, 256, (8, 16, C)); v[:, [1, 5, 7, 9, 11, 13, 15]] = 256
    tst[a] = v; th[a] = rng.integers(511, 1500, 8); th[b] = 0; th[d] = 0
    cov[b] = rng.integers(1, 256, (8, 16, W)); cov[d] = rng.integers(1, 256, (8, 16, W))
    c = np.arange(C); second = ((c % 2 == 0) & (c > 0)) | (c == C - 1)
    for g in range(8):
        p = np.append(rng.permutation(C - 1)[:31], C - 1)
        few = ((((2 * v[g, 2, p] + 1) * (2 * v[g, 3, p] + 1)) >> 4) + 613 * 2) & (W - 1)
        most = ((((2 * v[g, 3, p] + 1) * (2 * v[g, 4, p] + 1)) >> 4) + 613 * 3) & (W - 1)
        cov[a, g][:, few] = 255; cov[a, g][int(rng.integers(0, 16)), few] = 254; cov[a, g][:, most] = 255
        x, y, i = pairs(rng, 0)
        tst[b, g] = lone(rng, x[:C], y[:C], i[:C])
        x, y, i = pairs(rng, W - 254 if g == 7 else 0)
        o = (c + 1) // 2; o[C - 1] = 0; o = np.where(o > 0, 1 + (o - 1) % (len(x) - 1), 0)
        tst[d, g] = lone(rng, x[o], y[o], i[o])
        lev = rng.integers(0, 16, C // 2)[o]; lev = np.where(second, (lev + rng.integers(1, 16, C)) & 15, lev)
        pr[d, g] = np.where(np.arange(16)[:, None] == lev[None, :], 0, 255)
    return pack(cov, tst, pr, th)
def setup_inputs_ties(rng):
    unit = np.where(np.arange(8) % 4 == 1, 1, 85).reshape(1, 8, 1, 1)
    cov = unit * np.where(rng.random((N, 8, 1, W)) < 0.5, rng.integers(0, 4, (N, 8, 1, W)), rng.integers(0, 4, (N, 8, 16, W)))
    pr = unit * np.where(rng.random((N, 8, 1, C)) < 0.5, rng.integers(0, 2, (N, 8, 1, C)), rng.integers(0, 2, (N, 8, 16, C)))
    few = rng.choice(np.array([0, 1, 64, 128, 255, 256]), (N, 8, 16, C)); many = np.where(rng.random((N, 8, 16, C)) < 0.2, 256, rng.integers(0, 256, (N, 8, 16, C)))
    tst = np.where(rng.random((N, 8, 1, C)) < 0.5, few, many)
    return pack(cov, tst, pr, unit[..., 0, 0] * rng.integers(0, 24, (N, 8)))
def setup_inputs_spread(rng):
    cov = np.minimum((np.exp2(8 * rng.random((N, 8, 1, W))) * rng.random((N, 8, 16, W)) * 1.01).astype(np.int64), 255)
    pr = np.minimum((np.exp2(8 * rng.random((N, 8, 16, C))) * rng.random((N, 8, 1, C))).astype(np.int64), 255)
    tst = np.minimum((256 * rng.random((N, 8, 16, C)) ** rng.choice(np.array([0.25, 1.0, 4.0]), (N, 8, 16, 1))).astype(np.int64), 255)
    tst = np.where(rng.random((N, 8, 16, C)) < rng.random((N, 8, 1, C)) * 0.6, 256, tst)
    th = np.minimum(np.exp2(12 * rng.random((N, 8))).astype(np.int64) - 1, 4080)
    return pack(cov, tst, pr, th)
def setup_inputs_ends(rng):
    kind = rng.integers(0, 3, (N, 8, 1, W)); cov = 255 * np.where(kind == 2, rng.integers(0, 2, (N, 8, 16, W)), kind)
    lane = np.arange(16)
    for t in range(RO):
        z = (613 * lane + 77 * t) & (W - 1); f = ((511 * 511 >> 4) + 613 * lane + 77 * t) & (W - 1)
        cov[..., z] = 255; cov[..., f] = 0; cov[..., f[15]] = 255; cov[:, ::2, :, f[6]] = 255
    u = rng.random((N, 8, 16, C))
    tst = np.where(u < 0.5, 0, np.where(u < 0.7, 256, np.where(u < 0.9, 255, rng.integers(0, 256, (N, 8, 16, C)))))
    tst[..., [2, C - 1]] = 0; tst[..., [5, C - 2]] = 255; tst[..., [1, C - 3]] = 256
    pr = 255 * rng.integers(0, 2, (N, 8, 16, C))
    pr[..., [2, 5, C - 2, C - 1]] = 255; pr[:, :, 15, [2, 5, C - 2, C - 1]] = 0; pr[:, 1::2, 4, [2, C - 1]] = 0
    o = np.argsort(rng.random((N, 8)), axis=1); th = 4080 * (o < rng.integers(3, 6, (N, 1))).astype(np.int64)
    th[N - 1, 7] = 4080; th[N - 1, 0] = 0
    return pack(cov, tst, pr, th)
def check_inputs(d):
    bad = []
    for k, lo, hi in (("cov", 0, 255), ("tst", 0, 256), ("pr", 0, 255), ("th", 0, 4080)):
        v = np.asarray(d[k]).astype(np.float64)
        if not (np.min(v) >= lo and np.max(v) <= hi): bad.append("range of " + k)
        elif np.any(v != np.floor(v)): bad.append("whole numbers in " + k)
    return bad
def reference(cov, tst, pr, th):
    U = cov.astype(np.float32).astype(np.int64).reshape(N, 8, 16, W); T = tst.astype(np.int64).reshape(N, 8, 16, C)
    price = pr.astype(np.float32).astype(np.int64).reshape(N, 8, 16, C); lim = th.astype(np.int64).reshape(N, 8, 1)
    lane = np.arange(16).reshape(1, 16, 1); last = np.zeros(N, np.int64)
    for t in range(RO):
        rho = (5 * t) & 15; now = np.zeros(N, np.int64)
        for r in range(N):
            s = (r + t) % N
            x = T[r]; y = np.roll(x, -(1 + t), axis=1)
            live = (x != 256) & (y != 256)
            code = ((((2 * x + 1) * (2 * y + 1)) >> 4) + 613 * lane + 77 * t) & (W - 1)
            got = np.take_along_axis(U[s], code.reshape(8, 1, 16 * C), 2).reshape(8, 16, 16, C)
            gain = np.add.reduce(np.where(live[:, None], np.maximum(got - price[s][:, :, None, :], 0), 0), axis=2)
            lev = np.argmax(gain, axis=1); best = np.max(gain, axis=1)
            useful = best >= lim[s] + (last[s] & 255); now[s] = np.sum(~useful)
            some = np.any(live, axis=1)
            vote = np.argmax(np.where(live, np.add.reduce(got, axis=1), -1), axis=1)
            taken = np.take_along_axis(code, vote[:, None, :], 1)[:, 0] >> SH
            most = np.argmax(np.where(live, np.take_along_axis(got, lev[:, None, None, :], 1)[:, 0], -1), axis=1)
            credit = np.take_along_axis(code, most[:, None, :], 1)[:, 0]
            none = x == 256; first = np.argmax(none, axis=1)
            new = np.array(x)
            g, c = np.nonzero(~useful & some & np.any(none, axis=1))
            new[g, first[g, c], c] = taken[g, c]
            new[:, rho] = np.where(useful, 16 * lev + (best & 15), 256)
            for g in range(8):
                c = np.nonzero(useful[g] & some[g])[0]
                col, at = np.unique(credit[g, c], return_index=True)
                U[s, g, lev[g, c[at]], col] = 0
            T[r] = new
        last = now
    left = np.add.reduce(U.reshape(N, 128, W // 16, 16), axis=3)
    return {"yt": T.reshape(N, 128, C).astype(np.float32), "yc": left.astype(np.float32)}

@@ -1,0 +1,463 @@
+from concourse.mybir import AluOpType as A, AxisListType, ActivationFunctionType as F
+
+NONE = 2.0 ** 19
+W = 8192
+TR = 8192
+VOID = 8448
+UW = 8464
+SQ = 20480.0
+NF = 12
+RHO = [0, 5, 10, 15]
+
+SCRATCH = {}
+
+
+def _b(name, cols, dtype, where="sbuf"):
+    SCRATCH[name] = (where, [128] + (list(cols) if isinstance(cols, (list, tuple)) else [cols]), dtype)
+
+
+for _n, _c in (("U", UW), ("got", 4096), ("Mx", 4096), ("PX", 4096), ("D0C", 2048), ("D0G", 128), ("D0V", 128), ("segm", 256),
+               ("T0", 256), ("T1", 256), ("T2", 256), ("T3", 256), ("T4", 256), ("Tn0", 256), ("Tn1", 256), ("Tn2", 256), ("Tn3", 256),
+               ("Tt", 256), ("Nn", 256), ("prb", 256), ("hib", 256), ("FT", 256), ("rhs", 256), ("lhs", 256),
+               ("lhsE", 256), ("lhsO", 256), ("Xs", 256), ("vals", 256), ("mt0", 512), ("mt1", 512), ("mt2", 512), ("mt3", 512),
+               ("mt4", 512), ("mt5", 512), ("onesb", 256), ("I1", 128), ("I256", 128), ("nI", 128), ("Ind", 8), ("MQ", 256),
+               ("SEL", 240), ("CC", 128), ("CTa", 128), ("CTb", 128), ("CP", 128), ("CX", 128),
+               ("RT", 512), ("TNb", 128), ("TN", 512), ("CT", 512), ("FE", (2, 8 * NF))):
+    _b(_n, _c, "bfloat16")
+for _n, _c in (("xx", 256), ("pd", 256), ("GKs", (2, 128)), ("VKs", (2, 128)), ("ns", (2, 8)), ("us", (2, 8)), ("TH0", (2, 8)),
+               ("TH", (2, 8)), ("cnum", (2, 8)), ("Z", 256), ("M1", 256), ("L1", 256), ("dm", 256), ("D1", 256), ("l2f", 16),
+               ("BLK", 128), ("TM", 256), ("mif", 256), ("mf", 256), ("mgf", 128), ("w8", 8), ("colsf", 40), ("pw", 16), ("pw2", 16),
+               ("half", 16), ("msum", 4), ("yt32", 256), ("yc32", 512), ("mi2", 128), ("rowA", 128), ("rowB", 128), ("q1", 128),
+               ("q2", 128), ("s0", 128), ("s1", 128), ("s2", 128), ("s3", 128), ("sa", 128), ("sb", 128)):
+    _b(_n, _c, "float32")
+for _n, _c in (("tsti", 256), ("z", 256), ("ci", 256), ("hii", 256), ("GKi", (2, 8)), ("DEC", (2, 24)), ("VKi", (2, 8)), ("tki", (2, 8)),
+               ("A1", 256), ("A2", 256), ("thr", 8), ("thb", 8), ("mint", 4), ("mi", 128), ("ri", 512), ("pc", 8)):
+    _b(_n, _c, "int32")
+for _n, _c in (("K1", 4096), ("R", 256), ("If", 128), ("nIf", 128)):
+    _b(_n, _c, "float16")
+for _n, _c in (("off", 256), ("l1u", 16), ("l2u", 16)):
+    _b(_n, _c, "uint16")
+for _n in "ABCDEFGH":
+    _b("b" + _n, 512, "float32", "psum")
+
+SEMAPHORES = ["cv", "cs", "ct", "cg", "loc"] + ["d%d" % k for k in range(10)] + ["a%d" % k for k in range(1, 5)]
+
+
+def rank_program(g, core, T, topo):
+    rank = T.rank_of(core)
+    if rank is None:
+        return
+    N = len(T.cores)
+    eng = {"v": g.vector, "s": g.scalar, "t": g.tensor, "g": g, "y": g.sync}
+    cnt = {"v": 0, "s": 0, "t": 0, "g": 0}
+    known = {q: {} for q in eng}
+    clk = {}
+    wr, rd, bank = {}, {}, {}
+    ndma = [0]
+
+    def sem_of(e):
+        return T.sem["c" + e] if e in cnt else T.sem[e]
+
+    def need(q, deps):
+        best = {}
+        for e, n in deps:
+            if known[q].get(e, 0) < n and best.get(e, 0) < n:
+                best[e] = n
+        for e in list(best):
+            for e2 in list(best):
+                if e2 != e and e in best and e2 in best and clk.get((e2, best[e2]), {}).get(e, 0) >= best[e]:
+                    del best[e]
+        for e, n in best.items():
+            eng[q].wait_ge(sem_of(e), n)
+            for k, v in clk.get((e, n), {}).items():
+                if known[q].get(k, 0) < v:
+                    known[q][k] = v
+            known[q][e] = n
+
+    def deps_of(q, reads, writes):
+        deps = []
+        for t in list(reads) + list(writes):
+            if t[0] == "b":
+                for e, n in bank.get(t, {}).items():
+                    if e != q:
+                        deps.append((e, n))
+        for t in reads:
+            w = wr.get(t)
+            if w is not None and not (t[0] == "b" and w[0] != q):
+                deps.append(w)
+        for t in writes:
+            if t[0] != "b":
+                w = wr.get(t.rstrip("+"))
+                if w is not None and not (t[-1] == "+" and w[0] == q):
+                    deps.append(w)
+                deps.extend(rd.get(t.rstrip("+"), {}).items())
+        return deps
+
+    def note(q, e, n, reads, writes):
+        c = dict(known[q])
+        c[e] = n
+        clk[(e, n)] = c
+        for t in reads:
+            if t[0] == "b":
+                bank.setdefault(t, {})[e] = n
+            else:
+                rd.setdefault(t, {})[e] = n
+        for t in writes:
+            t = t.rstrip("+")
+            if t[0] == "b":
+                bank.setdefault(t, {})[e] = n
+            else:
+                rd[t] = {}
+            wr[t] = (e, n)
+
+    def op(q, fn, reads, writes):
+        reads = reads.split()
+        writes = writes.split()
+        need(q, deps_of(q, reads, writes))
+        ins = fn()
+        cnt[q] += 1
+        ins.then_inc(T.sem["c" + q], 1)
+        note(q, q, cnt[q], reads, writes)
+
+    def dma(q, out, in_, reads, writes):
+        reads = reads.split()
+        writes = writes.split()
+        need(q, deps_of("dma", reads, writes))
+        name = "d%d" % ndma[0]
+        ndma[0] += 1
+        eng[q].dma_start(out, in_).then_inc(T.sem[name], 16)
+        note(q, name, 16, reads, writes)
+
+    V, S, P = g.vector, g.scalar, g.tensor
+
+    def ts(out, in0, s1, s2, op0, op1, r, w):
+        if op1 is None:
+            op("v", lambda: V.tensor_scalar(out, in0, s1, None, op0), r, w)
+        else:
+            op("v", lambda: V.tensor_scalar(out, in0, s1, s2, op0, op1), r, w)
+
+    def tt(out, a, b, o, r, w):
+        op("v", lambda: V.tensor_tensor(out, a, b, o), r, w)
+
+    def cp(out, in_, r, w):
+        op("v", lambda: V.tensor_copy(out, in_), r, w)
+
+    def scan(out, d0, d1, o0, o1, r, w, init=0.0):
+        op("v", lambda: V.tensor_tensor_scan(out, d0, d1, init, o0, o1), r, w)
+
+    def act(out, in_, func, r, w, **k):
+        op("s", lambda: S.activation(out, in_, func, **k), r, w)
+
+    def mm(out, l, x, st, sp, r, w):
+        op("t", lambda: P.matmul(out, l, x, st, sp), r, w)
+
+    def ms(ap, c, w):
+        op("v", lambda: V.memset(ap, c), "", w)
+
+    def sel(out, in_, pat, cmp, fill, base, cm, r, w):
+        op("g", lambda: g.affine_select(out, in_, pat, cmp, fill, base, cm), r, w)
+
+    dma("y", T.tsti[:], T.tst[:], "", "tsti")
+    dma("y", T.thr[0:1, 0:8], T.th[:], "", "thr")
+    dma("s", T.prb[:], T.pr[:], "", "prb")
+    dma("y", T.U[:, 0:4096], T.cov[:, 0:4096], "", "Ua")
+    dma("s", T.U[:, 4096:W], T.cov[:, 4096:W], "", "Ub")
+    UALL = "Ua Ub Uc"
+
+    PI, PG, PP, OD, EV, SK, BK, CL, CR, N14, R14, R15, HB = range(13)
+    KC, RC_ = 16, 20
+    K = 8 * NF
+    BP = [[-1, 8], [0, 16]]
+    FL = {"allow_small_or_imprecise_dtypes": True}
+
+    def col(k):
+        return T.colsf[:, k:k + 1]
+
+    def iota(out, pat, base, cm, w, **k):
+        op("g", lambda: g.iota(out, pat, base, cm, **k), "", w)
+
+    iota(T.pc[:, 0:1], [[0, 1]], 0, 1, "pc0")
+    iota(T.ri[:, 0:128], [[1, 128]], 1, 0, "ri0")
+    iota(T.mgf[:], [[1, 8], [0, 16]], 0, 0, "mgf", **FL)
+    iota(col(PP), [[0, 1]], 0, 1, "f2", **FL)
+    iota(T.mif[:], [[0, 16], [1, 16]], 0, 0, "mif", **FL)
+    iota(T.mf[:], [[1, 256]], 0, 0, "mf", **FL)
+    op("g", lambda: g.partition_broadcast(T.thb[:], T.thr[0:1, 0:8], 128), "thr", "thb")
+    iota(T.w8[:], [[1, 8]], 0, 0, "w8", **FL)
+    iota(T.q1[:], [[0, 8], [-1, 16]], 7, 0, "q1", **FL)
+    iota(T.cnum[:], [[128, 2], [0, 8]], 0, 1, "cnum", **FL)
+
+    ms(T.onesb[:], 1.0, "onesb")
+    ts(T.pc[:, 1:2], T.pc[:, 0:1], 15, None, A.bitwise_and, None, "pc0", "pc1")
+    ts(T.pc[:, 2:3], T.pc[:, 0:1], 4, None, A.arith_shift_right, None, "pc0", "pc2")
+    ts(T.pc[:, 3:4], T.pc[:, 0:1], 4, 1, A.arith_shift_right, A.bitwise_and, "pc0", "pc3")
+    cp(col(PI), T.pc[:, 1:2], "pc1", "f0")
+    cp(col(PG), T.pc[:, 2:3], "pc2", "f1")
+    cp(col(OD), T.pc[:, 3:4], "pc3", "f3")
+    for t in range(4):
+        ts(col(KC + t), col(PI), 16.0 * 613, 16.0 * 77 * t, A.mult, A.add, "f0", "fk%d" % t)
+    ts(T.BLK[:], T.mgf[:], col(PG), None, A.is_equal, None, "mgf f1", "BLK")
+
+    def rot(t):
+        r, n = "ri%d" % t, "RT%d" % t
+        ts(T.mi[:], T.ri[:, 128 * t:128 * t + 128], 15, None, A.bitwise_and, None, r, "mi")
+        ts(T.mi2[:], T.mi[:], col(PI), 2.0, A.is_equal, A.mult, "mi f0", "mi2")
+        tt(T.RT[:, 128 * t:128 * t + 128], T.mi2[:], T.BLK[:], A.mult, "mi2 BLK", n)
+
+    def codes_start():
+        mm(T.bE[:, 0:256], T.onesb[0:1, 0:128], T.onesb[0:1, 0:256], True, False, "onesb", "bE")
+
+    def codes(t):
+        src = "T%d" % t
+        b = T[src]
+        mm(T.bE[:, 0:256], T.RT[:, 128 * t:128 * t + 128], b[:], False, True, "RT%d %s" % (t, src), "bE")
+        act(T.xx[:], b[:], F.Identity, src, "xx", scale=2.0, bias=1.0)
+        tt(T.pd[:], T.bE[:, 0:256], T.xx[:], A.mult, "bE xx", "pd")
+        ts(T.z[:], T.pd[:], col(KC + t), 2.0 ** 30, A.add, A.min, "pd fk%d" % t, "z")
+        ts(T.ci[:], T.z[:], 4, 8191 | 0x7FFF8000, A.arith_shift_right, A.bitwise_and, "z", "ci")
+        ts(T.off[:], T.ci[:], float(VOID), None, A.min, None, "ci", "off")
+
+    rot(0)
+    codes_start()
+    ts(T.pd[:], T.tsti[:], 256.0, NONE, A.is_ge, A.mult, "tsti", "pd")
+    tt(T.T0[:], T.pd[:], T.tsti[:], A.max, "pd tsti", "T0")
+    codes(0)
+    ms(T.U[:, W:VOID], 0.0, "Uc+")
+    ms(T.U[:, VOID:UW], -128.0, "Uc+")
+    for i in range(16):
+        if i < 12:
+            act(T.PX[:, i:4096:16], T.prb[:], F.Copy, "prb", "PXs+")
+        else:
+            cp(T.PX[:, i:4096:16], T.prb[:], "prb", "PXv+")
+    ts(T.s0[:], T.q1[:], 16384.0, None, A.mult, None, "q1", "s0")
+    ts(T.q2[:], T.q1[:], 16.0, None, A.add, None, "q1", "q2")
+    tt(T.q2[:], T.q2[:], T.q1[:], A.mult, "q1 q2", "q2")
+    ts(T.s1[:], T.q2[:], -8192.0, 8192.0, A.mult, A.add, "q2", "s1")
+    ts(T.s2[:], T.q1[:], -512.0, None, A.mult, None, "q1", "s2")
+    ts(T.s3[:], T.q2[:], 256.0, None, A.mult, None, "q2", "s3")
+    for n in ("CC", "CTa", "CTb"):
+        ms(T[n][:], 0.0, n)
+    m128 = T.mf[:, 0:128]
+    ts(T.I1[:], m128, col(PP), None, A.is_equal, None, "mf f2", "I1")
+    ts(T.I256[:], m128, col(PP), 256.0, A.is_equal, A.mult, "mf f2", "I256")
+    ts(T.nI[:], m128, col(PP), -4096.0, A.is_equal, A.mult, "mf f2", "nI")
+    ts(T.If[:], m128, col(PP), None, A.is_equal, None, "mf f2", "If")
+    ts(T.nIf[:], m128, col(PP), -1.0, A.is_equal, A.mult, "mf f2", "nIf")
+    ts(T.Ind[:], T.w8[:], col(PG), 256.0, A.is_equal, A.mult, "w8 f1", "Ind")
+    ts(T.segm[:], T.mif[:], 0.0, None, A.is_gt, None, "mif", "segm")
+    ts(T.rowA[:], m128, col(PP), NONE, A.is_gt, A.mult, "mf f2", "rowA")
+    ts(T.rowB[:], m128, col(PP), NONE, A.is_equal, A.mult, "mf f2", "rowB")
+    tt(T.rowA[:], T.rowA[:], T.rowB[:], A.subtract, "rowA rowB", "rowA")
+    tt(T.TNb[:], T.rowA[:], T.BLK[:], A.mult, "rowA BLK", "TNb")
+    for k in range(8):
+        ts(T.D0C[:, 256 * k:256 * k + 256], T.segm[:], 2.0 ** 20 + 1, -2.0 ** 20, A.mult, A.add, "segm", "D0C+")
+    ts(T.D0G[:], T.segm[:, 0:128], 2.0 ** 25 + 16, -2.0 ** 25, A.mult, A.add, "segm", "D0G")
+    ts(T.D0V[:], T.segm[:, 0:128], 2.0 ** 27 + 256, -2.0 ** 27, A.mult, A.add, "segm", "D0V")
+    for h in range(2):
+        ts(T.TH0[:, h, :], T.thb[:], 256.0, -SQ, A.mult, A.add, "thb", "TH0+")
+    for t in range(4):
+        ts(col(RC_ + t), col(PI), float(RHO[t]), NONE, A.is_equal, A.mult, "f0", "fr%d" % t)
+
+    def fills(n, items):
+        for f, v in items:
+            sel(T[n][0:K, :], T[n][0:K, :], BP, A.not_equal, v, -8 * f, 1, n, n)
+
+    def tn(t):
+        sel(T.TN[:, 128 * t:128 * t + 128], T.TNb[:], [[0, 8], [1, 16]], A.not_equal, 0.0, -RHO[t], 0, "TNb", "TN%d" % t)
+
+    def ctg(t):
+        sel(T.sa[0:K, :], T.CTa[0:K, :], [[0, 8], [1, 16]], A.not_equal, 0.0, -RHO[t], 0, "CTa", "sa")
+        sel(T.sb[0:K, :], T.CTb[0:K, :], [[0, 8], [1, 16]], A.is_equal, 0.0, -RHO[t], 0, "CTb", "sb")
+
+    def ctv(t):
+        tt(T.CT[0:K, 128 * t:128 * t + 128], T.sa[0:K, :], T.sb[0:K, :], A.add, "sa sb", "CT%d" % t)
+
+    sel(T.s0[0:K, :], T.s0[0:K, :], BP, A.is_equal, 0.0, -8 * 2, 1, "s0", "s0")
+    sel(T.s1[0:K, :], T.s1[0:K, :], BP, A.is_equal, 0.0, -8 * 11, 1, "s1", "s1")
+    fills("s0", [(5, -8192.0), (7, -8192.0)])
+    fills("CTa", [(10, 1.0), (9, NONE), (11, NONE)])
+    fills("CTb", [(0, -16.0), (1, 1.0), (6, NONE), (11, 240.0)])
+    tn(0)
+    ctg(0)
+    sel(T.s2[0:K, :], T.s2[0:K, :], BP, A.is_equal, 0.0, 0, 1, "s2", "s2")
+    sel(T.s3[0:K, :], T.s3[0:K, :], BP, A.is_equal, 0.0, -8 * 11, 1, "s3", "s3")
+    fills("s2", [(3, 256.0)])
+    fills("CC", [(5, 2.0 ** 17), (2, 2.0 ** 17), (7, 2.0 ** 17), (8, 1.0), (11, 201.0 * 8192)])
+    for t in range(1, 4):
+        iota(T.ri[:, 128 * t:128 * t + 128], [[1, 128]], 1 + t, 0, "ri%d" % t)
+
+    ts(T.MQ[:], T.mif[:], col(PI), None, A.is_equal, None, "mif f0", "MQ")
+    ts(T.TM[:], T.mf[:], float(TR), None, A.add, None, "mf", "TM")
+    tt(T.TM[:], T.TM[:], T.MQ[:], A.mult, "TM MQ", "TM")
+    ts(col(EV), col(OD), -1.0, 1.0, A.mult, A.add, "f3", "f4")
+    ms(T.SEL[:, 0:112], 0.0, "SEL+")
+    ms(T.SEL[:, 128:240], 0.0, "SEL+")
+    ms(T.SEL[:, 112:128], 2.0 ** 24, "SEL+")
+    ms(T.FE[:], 1.0, " ".join("F%d" % k for k in range(NF)))
+    ms(T.half[:], 0.5, "half")
+    ms(T.pw2[:], 0.0, "pw2")
+    scan(T.pw[:], T.half[:], T.pw2[:], A.mult, A.add, "half pw2", "pw", 2.0)
+    ts(T.pw2[:], T.mif[:, 0:16], col(PI), None, A.is_equal, None, "mif f0", "pw2")
+    tt(T.pw[:], T.pw[:], T.pw2[:], A.mult, "pw pw2", "pw")
+    op("v", lambda: V.tensor_reduce(col(SK), T.pw[:, 0:14], AxisListType.X, A.add), "pw", "f5")
+    ts(col(BK), col(SK), 0.5, -0.5, A.mult, A.add, "f5", "f6")
+    ts(col(R14), col(PI), 14.0, None, A.is_equal, None, "f0", "f10")
+    ts(col(R15), col(PI), 15.0, None, A.is_equal, None, "f0", "f11")
+    ts(col(HB), col(PI), 14.0, 0.5, A.is_lt, A.mult, "f0", "f12")
+    tt(col(CL), col(HB), col(R14), A.subtract, "f12 f10", "f7")
+    tt(col(CR), col(HB), col(R15), A.subtract, "f12 f11", "f8")
+    ts(col(N14), col(R14), -1.0, None, A.mult, None, "f10", "f9")
+    ts(T.dm[:], T.mf[:], 1.0 / 1024, None, A.mult, None, "mf", "dm")
+    ts(T.bH[:, 0:256], T.dm[:], col(R15), col(CL), A.mult, A.add, "dm f11 f7", "bH")
+    ts(T.bH[:, 256:512], T.dm[:], col(N14), col(CR), A.mult, A.add, "dm f9 f8", "bH")
+
+    def fe(f, n=1):
+        return T.FE[:, :, 8 * f:8 * (f + n)]
+
+    ALLF = " ".join("F%d" % k for k in range(NF))
+    GB, VB = [T.bA, T.bB], [T.bC, T.bD]
+    GN, VN = ["bA", "bB"], ["bC", "bD"]
+    win = T.U[:, 0:UW]
+    FT = T.FT[0:K, :]
+
+    for t in range(4):
+        src = "T%d" % t
+        for h in range(2):
+            a, b = 2048 * h, 2048 * h + 2048
+            o = T.off[:, 128 * h:128 * h + 128]
+            act(T.got[:, a:b], win.indirect(o), F.Identity, "off " + UALL, "got%d" % h, scale=16.0, bias=-2048.0)
+            op("v", lambda: V.tensor_tensor(T.Mx[:, a:b], win.indirect(o), T.PX[:, a:b], A.max), "off PXs PXv " + UALL, "Mx%d" % h)
+            if h == 0:
+                ts(T.hii[:], T.z[:], 9, 255, A.arith_shift_right, A.bitwise_and, "z", "hii")
+                ts(T.Nn[:], T[src][:], NONE / 2, None, A.is_ge, None, src, "Nn")
+                ts(T.Tt[:], T[src][:], col(RC_ + t), None, A.max, None, src + " fr%d" % t, "Tt")
+                cp(T.hib[:], T.hii[:], "hii", "hib")
+            mm(GB[h][:, 0:128], T.prb[:, 128 * h:128 * h + 128], T.nI[:], True, False, "prb nI", GN[h])
+            for i in range(16):
+                mm(GB[h][:, 0:128], T.Mx[:, a + i:b:16], T.I256[:], False, False, "Mx%d I256" % h, GN[h])
+            mm(VB[h][:, 0:128], T.hib[:, 128 * h:128 * h + 128], T.I1[:], True, False, "hib I1", VN[h])
+            for i in range(16):
+                mm(VB[h][:, i:128:16], T.got[:, a + i:b:16], T.Ind[:], False, i == 15, "got%d Ind" % h, VN[h])
+        mm(T.bF[:, 0:256], T.TN[:, 128 * t:128 * t + 128], T.Nn[:], True, False, "TN%d Nn" % t, "bF")
+        for h in range(2):
+            a, b = 2048 * h, 2048 * h + 2048
+            scan(T.K1[:, a:b], T.D0C[:], T.got[:, a:b], A.add, A.max, "D0C got%d" % h, "K1%d" % h)
+        if t == 0:
+            tt(T.CP[0:K, :], T.s0[0:K, :], T.s1[0:K, :], A.add, "s0 s1", "CP")
+            tt(T.CX[0:K, :], T.s2[0:K, :], T.s3[0:K, :], A.add, "s2 s3", "CX")
+        ctv(t)
+        ts(T.R[:], T.K1[:, 15:4096:16], SQ - 7.5, None, A.add, None, "K10 K11", "R")
+        for h in range(2):
+            mm(GB[h][:, 0:128], T.K1[:, 2048 * h + 15:2048 * h + 2048:16], T.If[:], False, False, "K1%d If" % h, GN[h])
+            mm(GB[h][:, 0:128], T.R[:, 128 * h:128 * h + 128], T.nIf[:], False, True, "R nIf", GN[h])
+        for h in range(2):
+            scan(T.VKs[:, h, :], T.D0V[:], VB[h][:, 0:128], A.add, A.max, "D0V " + VN[h], "VKs+")
+        vk = T.VKs[:, :, 15:128:16]
+        ts(T.VKi[:], vk, 2.0 ** 23, None, A.add, None, "VKs", "VKi")
+        ts(T.ns[:], vk, -2.0 ** 23, None, A.is_lt, None, "VKs", "ns")
+        ts(T.tki[:], T.VKi[:], 255, None, A.bitwise_and, None, "VKi", "tki")
+        cp(fe(10), T.tki[:], "tki", "F10")
+        for h in range(2):
+            scan(T.GKs[:, h, :], T.D0G[:], GB[h][:, 0:128], A.add, A.max, "D0G " + GN[h], "GKs+")
+        gk = T.GKs[:, :, 15:128:16]
+        th = T.TH0 if t == 0 else T.TH
+        thn = "TH0" if t == 0 else "TH"
+        ts(T.GKi[:], gk, SQ, None, A.add, None, "GKs", "GKi")
+        tt(fe(6), gk, th[:], A.is_lt, "GKs " + thn, "F6")
+        tt(T.us[:], gk, th[:], A.is_ge, "GKs " + thn, "us")
+        ts(T.DEC[:, :, 0:8], T.GKi[:], 4, 15, A.arith_shift_right, A.bitwise_and, "GKi", "DEC0")
+        ts(T.DEC[:, :, 8:16], T.GKi[:], 8, 15, A.arith_shift_right, A.bitwise_and, "GKi", "DEC1")
+        ts(T.DEC[:, :, 16:24], T.GKi[:], 15, None, A.bitwise_and, None, "GKi", "DEC2")
+        tt(fe(7), fe(6), T.ns[:], A.max, "F6 ns", "F7")
+        cp(fe(0, 3), T.DEC[:], "DEC0 DEC1 DEC2", "F0 F1 F2")
+        act(fe(3, 3), fe(0, 3), F.Square, "F0 F1 F2", "F3 F4 F5", bias=-8.0)
+        tt(fe(8), fe(7), T.cnum[:], A.mult, "F7 cnum", "F8")
+        tt(fe(9), T.us[:], T.ns[:], A.max, "us ns", "F9")
+        for h in range(2):
+            mm(T.bE[0:K, 128 * h:128 * h + 128], T.FE[:, h, :], T.I1[:], True, True, ALLF + " I1", "bE")
+        act(FT, T.bE[0:K, 0:256], F.Copy, "bE", "FT")
+        mm(T.bG[:, 0:256], T.CP[0:K, :], FT, True, True, "CP FT", "bG")
+        mm(T.bF[:, 0:256], T.CT[0:K, 128 * t:128 * t + 128], FT, False, True, "CT%d FT" % t, "bF")
+        mm(T.bE[:, 256:512], T.CX[0:K, :], FT, True, True, "CX FT", "bE")
+        tt(T.Z[:], T.bG[:, 0:256], T.ci[:], A.min, "bG ci", "Z")
+        mm(T.bG[:, 256:512], T.CC[0:K, :], FT, True, False, "CC FT", "bG")
+        mm(T.bG[:, 256:512], T.BLK[:], T.Z[:], False, True, "BLK Z", "bG")
+        tt(T["Tn%d" % t][:], T.bF[:, 0:256], T.Tt[:], A.min, "bF Tt", "Tn%d" % t)
+        act(T.Xs[:], T.bE[:, 256:512], F.Copy, "bE", "Xs")
+        dst = T.cores[(rank + 1) % N] if t < 3 else T.cores[(rank - 3) % N]
+        es = topo.engines(core, dst)[::2]
+        need("g", deps_of("g", ["Tn%d" % t], []))
+        rid, pid, _s = topo.addr(dst)
+        g.remote_dma(T["T%d" % (t + 1)][:], T["Tn%d" % t][:], T.sem["a%d" % (t + 1)], T.sem.loc, pid, rid, sum(1 << e for e in es))
+        wr["T%d" % (t + 1)] = ("a%d" % (t + 1), len(es))
+        nloc = len(es)
+        if t < 3:
+            tn(t + 1)
+            ctg(t + 1)
+        colA = T.bG[:, 256:512]
+        ts(T.A1[:], colA, col(SK), col(BK), A.mult, A.add, "bG f5 f6", "A1")
+        ts(T.A2[:], T.A1[:], 1, None, A.bitwise_and, None, "A1", "A2")
+        tt(T.lhs[:], T.A2[:], T.bH[:, 0:256], A.subtract, "A2 bH", "lhs")
+        tt(T.rhs[:], T.A2[:], T.bH[:, 256:512], A.subtract, "A2 bH", "rhs")
+        ts(T.lhsE[:], T.lhs[:], col(EV), None, A.mult, None, "lhs f4", "lhsE")
+        ts(T.lhsO[:], T.lhs[:], col(OD), None, A.mult, None, "lhs f3", "lhsO")
+
+        def gram(bn, pos, gr, half):
+            ba = 32 * (gr // 2)
+            l = T.lhsE if gr % 2 == 0 else T.lhsO
+            ln = "lhsE" if gr % 2 == 0 else "lhsO"
+            n, c0 = (256, 0) if half == 0 else (128, 128)
+            mm(T[bn][:, pos:pos + n], l[ba:ba + 32, c0:c0 + 128], T.rhs[ba:ba + 32, c0:256], True, True, ln + " rhs", bn)
+
+        for k, bn in enumerate(("bA", "bB", "bC", "bD")):
+            gram(bn, 0, 2 * k, 0)
+            gram(bn, 256, 2 * k + 1, 0)
+        last = {}
+        for bn, pair in (("bE", 0), ("bF", 2), ("bE", 1), ("bF", 3)):
+            if bn in last:
+                need("t", [("t", last[bn])])
+            for k in range(2):
+                gram(bn, 256 * (pair % 2) + 128 * k, 2 * pair + k, 1)
+            last[bn] = cnt["t"]
+        tt(T.M1[:], colA, T.MQ[:], A.mult, "bG MQ", "M1")
+        scan(T.L1[:], T.segm[:], T.M1[:], A.mult, A.add, "segm M1", "L1")
+        cp(T.l1u[:], T.L1[:, 15:256:16], "L1", "l1u")
+        op("v", lambda: V.tensor_tensor(T.vals[:], win.indirect(T.l1u[:]), T.Xs[:], A.min), "l1u Xs " + UALL, "vals")
+        for k, bn, q in ((0, "bA", "s"), (1, "bB", "s"), (2, "bC", "v"), (3, "bD", "s"), (4, "bE", "v"), (5, "bF", "s")):
+            mt = T["mt%d" % k]
+            if q == "s":
+                act(mt[:], T[bn][:], F.Relu, bn, "mt%d" % k, bias=-3.5)
+            else:
+                ts(mt[:], T[bn][:], -3.5, 0.0, A.add, A.max, bn, "mt%d" % k)
+        if t < 3:
+            for h in range(2):
+                mm(T.bF[:, 256 + 8 * h:264 + 8 * h], T.onesb[:, 0:128], T.FE[:, h, 48:56], True, True, "onesb F6", "bF")
+            op("v", lambda: V.tensor_reduce(T.msum[:, 0:1], T.bF[:, 256:272], AxisListType.X, A.add), "bF", "msum0")
+            cp(T.mint[:, 0:1], T.msum[:, 0:1], "msum0", "mint0")
+            ts(T.mint[:, 1:2], T.mint[:, 0:1], 255, None, A.bitwise_and, None, "mint0", "mint1")
+            ts(T.msum[:, 1:2], T.mint[:, 1:2], 256.0, None, A.mult, None, "mint1", "msum1")
+            ts(T.TH[:], T.TH0[:], T.msum[:, 1:2], None, A.add, None, "TH0 msum1", "TH")
+            rot(t + 1)
+            codes_start()
+            codes(t + 1)
+        for gr in range(8):
+            mm(T.bG[:, 0:256], T.SEL[:, 112 - 16 * gr:240 - 16 * gr], T["mt%d" % (gr // 2)][:, 256 * (gr % 2):256 * (gr % 2) + 256],
+               gr == 0, False, "SEL mt%d" % (gr // 2), "bG")
+        for gr in range(8):
+            mm(T.bG[:, 128:256], T.SEL[:, 112 - 16 * gr:240 - 16 * gr], T["mt%d" % (4 + gr // 4)][:, 128 * (gr % 4):128 * (gr % 4) + 128],
+               False, gr == 7, "SEL mt%d" % (4 + gr // 4), "bG")
+        tt(T.dm[:], T.bG[:, 0:256], T.TM[:], A.min, "bG TM", "dm")
+        scan(T.D1[:], T.segm[:], T.dm[:], A.mult, A.add, "segm dm", "D1")
+        tt(T.l2f[:], T.L1[:, 15:256:16], T.D1[:, 15:256:16], A.max, "L1 D1", "l2f")
+        cp(T.l2u[:], T.l2f[:], "l2f", "l2u")
+        op("v", lambda: V.tensor_copy(win.indirect(T.l2u[:]), T.vals[:]), "l2u vals", UALL)
+
+    ts(T.yt32[:], T.T4[:], 256.0, None, A.min, None, "T4", "yt32")
+    dma("y", T.yt[:], T.yt32[:], "yt32", "yt")
+    for k in range(16):
+        mm(T.bA[:], T.I1[:], T.U[:, k:W:16], k == 0, k == 15, "I1 " + UALL, "bA")
+    act(T.yc32[:], T.bA[:], F.Copy, "bA", "yc32")
+    dma("y", T.yc[:], T.yc32[:], "yc32", "yc")
+    fin = [(q, n) for q, n in cnt.items() if n] + [("d%d" % k, 16) for k in range(ndma[0])]
+    need("g", fin)
+    g.wait_ge(T.sem.loc, 4 * nloc)

@@ -6,7 +6,8 @@ TR = 8192
 VOID = 8448
 UW = 8464
 SQ = 20480.0
-NF = 12
+NS = 32
+K1R, K2R = 56, 48
 RHO = [0, 5, 10, 15]
 
 SCRATCH = {}
@@ -16,24 +17,24 @@ def _b(name, cols, dtype, where="sbuf"):
     SCRATCH[name] = (where, [128] + (list(cols) if isinstance(cols, (list, tuple)) else [cols]), dtype)
 
 
-for _n, _c in (("U", UW), ("got", 4096), ("Mx", 4096), ("PX", 4096), ("D0C", 2048), ("D0G", 128), ("D0V", 128), ("segm", 256),
+for _n, _c in (("U", UW), ("got", 4096), ("Mx", 4096), ("PX", 4096), ("D0C", 1024), ("D0G", 128), ("D0V", 128), ("segm", 256),
                ("T0", 256), ("T1", 256), ("T2", 256), ("T3", 256), ("T4", 256), ("Tn0", 256), ("Tn1", 256), ("Tn2", 256), ("Tn3", 256),
-               ("Tt", 256), ("Nn", 256), ("prb", 256), ("hib", 256), ("FT", 256), ("rhs", 256), ("lhs", 256),
+               ("Tt", 256), ("Nn", 256), ("prb", 256), ("prb2", 128), ("FT", 256), ("FT2", 256), ("rhs", 256), ("lhs", 256),
                ("lhsE", 256), ("lhsO", 256), ("Xs", 256), ("vals", 256), ("mt0", 512), ("mt1", 512), ("mt2", 512), ("mt3", 512),
-               ("mt4", 512), ("mt5", 512), ("onesb", 256), ("I1", 128), ("I256", 128), ("nI", 128), ("Ind", 8), ("MQ", 256),
-               ("SEL", 240), ("CC", 128), ("CTa", 128), ("CTb", 128), ("CP", 128), ("CX", 128),
-               ("RT", 512), ("TNb", 128), ("TN", 512), ("CT", 512), ("FE", (2, 8 * NF))):
+               ("mt4", 512), ("mt5", 512), ("onesb", 256), ("I1", 128), ("I256", 128), ("nI", 128), ("nI16", 128), ("Ind", 8), ("MQ", 256),
+               ("SEL", 240), ("CC", 128), ("CTa", 128), ("CP", 128), ("CX", 128), ("zb", 128), ("m16", 4),
+               ("RT", 512), ("TNb", 128), ("TN", 512), ("CT", 512), ("FE", (2, K1R)), ("FE2", (2, K2R))):
     _b(_n, _c, "bfloat16")
-for _n, _c in (("xx", 256), ("pd", 256), ("GKs", (2, 128)), ("VKs", (2, 128)), ("ns", (2, 8)), ("us", (2, 8)), ("TH0", (2, 8)),
-               ("TH", (2, 8)), ("cnum", (2, 8)), ("Z", 256), ("M1", 256), ("L1", 256), ("dm", 256), ("D1", 256), ("l2f", 16),
+for _n, _c in (("xx", 256), ("pd", 256), ("GKs", (2, 128)), ("VKs", (2, 128)), ("TH0", (2, 8)),
+               ("TH", (2, 8)), ("Z", 256), ("M1", 256), ("L1", 256), ("dm", 256), ("D1", 256), ("l2f", 16),
                ("BLK", 128), ("TM", 256), ("mif", 256), ("mf", 256), ("mgf", 128), ("w8", 8), ("colsf", 40), ("pw", 16), ("pw2", 16),
-               ("half", 16), ("msum", 4), ("yt32", 256), ("yc32", 512), ("mi2", 128), ("rowA", 128), ("rowB", 128), ("q1", 128),
-               ("q2", 128), ("s0", 128), ("s1", 128), ("s2", 128), ("s3", 128), ("sa", 128), ("sb", 128)):
+               ("half", 16), ("msum", 4), ("junk", 16), ("yt32", 256), ("yc32", 512), ("ysc", 2048), ("mi2", 128), ("rowA", 128),
+               ("rowB", 128), ("q1", 128), ("q2", 128), ("s0", 128), ("s1", 128), ("s2", 128), ("s3", 128)):
     _b(_n, _c, "float32")
-for _n, _c in (("tsti", 256), ("z", 256), ("ci", 256), ("hii", 256), ("GKi", (2, 8)), ("DEC", (2, 24)), ("VKi", (2, 8)), ("tki", (2, 8)),
-               ("A1", 256), ("A2", 256), ("thr", 8), ("thb", 8), ("mint", 4), ("mi", 128), ("ri", 512), ("pc", 8)):
+for _n, _c in (("tsti", 256), ("z", 256), ("ci", 256), ("GKi", (2, 8)), ("DEC", (2, 24)), ("VKi", (2, 8)), ("tki", (2, 8)),
+               ("A1", 256), ("A2", 256), ("thr", 8), ("thb", 8), ("mi", 128), ("ri", 128), ("pc", 8)):
     _b(_n, _c, "int32")
-for _n, _c in (("K1", 4096), ("R", 256), ("If", 128), ("nIf", 128)):
+for _n, _c in (("K1", 4096), ("R", 256), ("If", 128), ("nIf", 128), ("hib", 256)):
     _b(_n, _c, "float16")
 for _n, _c in (("off", 256), ("l1u", 16), ("l2u", 16)):
     _b(_n, _c, "uint16")
@@ -158,15 +159,14 @@ def rank_program(g, core, T, topo):
         op("g", lambda: g.affine_select(out, in_, pat, cmp, fill, base, cm), r, w)
 
     dma("y", T.tsti[:], T.tst[:], "", "tsti")
-    dma("y", T.thr[0:1, 0:8], T.th[:], "", "thr")
     dma("s", T.prb[:], T.pr[:], "", "prb")
+    dma("y", T.thr[0:1, 0:8], T.th[:], "", "thr")
     dma("y", T.U[:, 0:4096], T.cov[:, 0:4096], "", "Ua")
     dma("s", T.U[:, 4096:W], T.cov[:, 4096:W], "", "Ub")
     UALL = "Ua Ub Uc"
 
-    PI, PG, PP, OD, EV, SK, BK, CL, CR, N14, R14, R15, HB = range(13)
+    PI, PG, PP, OD, EV, SK, BK, CL, CR, N14, R14, R15, HB, PH = range(14)
     KC, RC_ = 16, 20
-    K = 8 * NF
     BP = [[-1, 8], [0, 16]]
     FL = {"allow_small_or_imprecise_dtypes": True}
 
@@ -177,212 +177,263 @@ def rank_program(g, core, T, topo):
         op("g", lambda: g.iota(out, pat, base, cm, **k), "", w)
 
     iota(T.pc[:, 0:1], [[0, 1]], 0, 1, "pc0")
-    iota(T.ri[:, 0:128], [[1, 128]], 1, 0, "ri0")
+    iota(T.ri[:], [[1, 128]], 1, 0, "ri")
     iota(T.mgf[:], [[1, 8], [0, 16]], 0, 0, "mgf", **FL)
     iota(col(PP), [[0, 1]], 0, 1, "f2", **FL)
-    iota(T.mif[:], [[0, 16], [1, 16]], 0, 0, "mif", **FL)
+    iota(col(PH), [[0, 1]], 128, 1, "f13", **FL)
     iota(T.mf[:], [[1, 256]], 0, 0, "mf", **FL)
-    op("g", lambda: g.partition_broadcast(T.thb[:], T.thr[0:1, 0:8], 128), "thr", "thb")
+    iota(T.mif[:], [[0, 16], [1, 16]], 0, 0, "mif", **FL)
     iota(T.w8[:], [[1, 8]], 0, 0, "w8", **FL)
     iota(T.q1[:], [[0, 8], [-1, 16]], 7, 0, "q1", **FL)
-    iota(T.cnum[:], [[128, 2], [0, 8]], 0, 1, "cnum", **FL)
+    op("g", lambda: g.partition_broadcast(T.thb[:], T.thr[0:1, 0:8], 128), "thr", "thb")
 
     ms(T.onesb[:], 1.0, "onesb")
+    ms(T.zb[:], 0.0, "zb")
+    ms(T.CTa[:], 0.0, "CTa")
+    ms(T.CC[:], 0.0, "CC")
     ts(T.pc[:, 1:2], T.pc[:, 0:1], 15, None, A.bitwise_and, None, "pc0", "pc1")
     ts(T.pc[:, 2:3], T.pc[:, 0:1], 4, None, A.arith_shift_right, None, "pc0", "pc2")
     ts(T.pc[:, 3:4], T.pc[:, 0:1], 4, 1, A.arith_shift_right, A.bitwise_and, "pc0", "pc3")
     cp(col(PI), T.pc[:, 1:2], "pc1", "f0")
     cp(col(PG), T.pc[:, 2:3], "pc2", "f1")
     cp(col(OD), T.pc[:, 3:4], "pc3", "f3")
-    for t in range(4):
-        ts(col(KC + t), col(PI), 16.0 * 613, 16.0 * 77 * t, A.mult, A.add, "f0", "fk%d" % t)
     ts(T.BLK[:], T.mgf[:], col(PG), None, A.is_equal, None, "mgf f1", "BLK")
+    ts(T.mi[:], T.ri[:], 15, None, A.bitwise_and, None, "ri", "mi")
+    ts(T.mi2[:], T.mi[:], col(PI), 2.0, A.is_equal, A.mult, "mi f0", "mi2")
+    tt(T.RT[:, 0:128], T.mi2[:], T.BLK[:], A.mult, "mi2 BLK", "RT0")
 
     def rot(t):
-        r, n = "ri%d" % t, "RT%d" % t
-        ts(T.mi[:], T.ri[:, 128 * t:128 * t + 128], 15, None, A.bitwise_and, None, r, "mi")
-        ts(T.mi2[:], T.mi[:], col(PI), 2.0, A.is_equal, A.mult, "mi f0", "mi2")
-        tt(T.RT[:, 128 * t:128 * t + 128], T.mi2[:], T.BLK[:], A.mult, "mi2 BLK", n)
+        s, n = 1 + t, "RT%d" % t
+        b = T.RT[:, 128 * t:128 * t + 128]
+        sel(b, T.zb[:], [[-16, 8], [-1, 16]], A.not_equal, 2.0, -s, 1, "zb", n)
+        sel(b, b, [[-16, 8], [-1, 16]], A.not_equal, 2.0, 16 - s, 1, n, n)
+        sel(b, b, [[-16, 8], [0, 16]], A.is_ge, 0.0, 0, 1, n, n)
+        sel(b, b, [[16, 8], [0, 16]], A.is_ge, 0.0, 15, -1, n, n)
 
     def codes_start():
-        mm(T.bE[:, 0:256], T.onesb[0:1, 0:128], T.onesb[0:1, 0:256], True, False, "onesb", "bE")
+        mm(T.bA[:, 0:256], T.onesb[0:1, 0:128], T.onesb[0:1, 0:256], True, False, "onesb", "bA")
+
+    def codes_y(t):
+        src = "T%d" % t
+        mm(T.bA[:, 0:256], T.RT[:, 128 * t:128 * t + 128], T[src][:], False, True, "RT%d %s" % (t, src), "bA")
+
+    def codes_x(t):
+        src = "T%d" % t
+        act(T.xx[:], T[src][:], F.Identity, src, "xx", scale=2.0, bias=1.0)
 
     def codes(t):
-        src = "T%d" % t
-        b = T[src]
-        mm(T.bE[:, 0:256], T.RT[:, 128 * t:128 * t + 128], b[:], False, True, "RT%d %s" % (t, src), "bE")
-        act(T.xx[:], b[:], F.Identity, src, "xx", scale=2.0, bias=1.0)
-        tt(T.pd[:], T.bE[:, 0:256], T.xx[:], A.mult, "bE xx", "pd")
+        tt(T.pd[:], T.bA[:, 0:256], T.xx[:], A.mult, "bA xx", "pd")
         ts(T.z[:], T.pd[:], col(KC + t), 2.0 ** 30, A.add, A.min, "pd fk%d" % t, "z")
         ts(T.ci[:], T.z[:], 4, 8191 | 0x7FFF8000, A.arith_shift_right, A.bitwise_and, "z", "ci")
         ts(T.off[:], T.ci[:], float(VOID), None, A.min, None, "ci", "off")
 
-    rot(0)
     codes_start()
-    ts(T.pd[:], T.tsti[:], 256.0, NONE, A.is_ge, A.mult, "tsti", "pd")
-    tt(T.T0[:], T.pd[:], T.tsti[:], A.max, "pd tsti", "T0")
-    codes(0)
-    ms(T.U[:, W:VOID], 0.0, "Uc+")
-    ms(T.U[:, VOID:UW], -128.0, "Uc+")
-    for i in range(16):
-        if i < 12:
-            act(T.PX[:, i:4096:16], T.prb[:], F.Copy, "prb", "PXs+")
-        else:
-            cp(T.PX[:, i:4096:16], T.prb[:], "prb", "PXv+")
-    ts(T.s0[:], T.q1[:], 16384.0, None, A.mult, None, "q1", "s0")
-    ts(T.q2[:], T.q1[:], 16.0, None, A.add, None, "q1", "q2")
-    tt(T.q2[:], T.q2[:], T.q1[:], A.mult, "q1 q2", "q2")
-    ts(T.s1[:], T.q2[:], -8192.0, 8192.0, A.mult, A.add, "q2", "s1")
-    ts(T.s2[:], T.q1[:], -512.0, None, A.mult, None, "q1", "s2")
-    ts(T.s3[:], T.q2[:], 256.0, None, A.mult, None, "q2", "s3")
-    for n in ("CC", "CTa", "CTb"):
-        ms(T[n][:], 0.0, n)
     m128 = T.mf[:, 0:128]
     ts(T.I1[:], m128, col(PP), None, A.is_equal, None, "mf f2", "I1")
     ts(T.I256[:], m128, col(PP), 256.0, A.is_equal, A.mult, "mf f2", "I256")
-    ts(T.nI[:], m128, col(PP), -4096.0, A.is_equal, A.mult, "mf f2", "nI")
-    ts(T.If[:], m128, col(PP), None, A.is_equal, None, "mf f2", "If")
-    ts(T.nIf[:], m128, col(PP), -1.0, A.is_equal, A.mult, "mf f2", "nIf")
-    ts(T.Ind[:], T.w8[:], col(PG), 256.0, A.is_equal, A.mult, "w8 f1", "Ind")
+    ts(T.pd[:], T.tsti[:], 256.0, NONE, A.is_ge, A.mult, "tsti", "pd")
+    tt(T.T0[:], T.pd[:], T.tsti[:], A.max, "pd tsti", "T0")
+    codes_y(0)
+    codes_x(0)
+    for t in range(4):
+        ts(col(KC + t), col(PI), 16.0 * 613, 16.0 * 77 * t, A.mult, A.add, "f0", "fk%d" % t)
     ts(T.segm[:], T.mif[:], 0.0, None, A.is_gt, None, "mif", "segm")
+    codes(0)
+    for i in range(16):
+        if i < 6:
+            act(T.PX[:, i:4096:16], T.prb[:], F.Copy, "prb", "PXs+")
+        else:
+            cp(T.PX[:, i:4096:16], T.prb[:], "prb", "PXv+")
+    act(T.s0[:], T.q1[:], F.Copy, "q1", "s0", scale=16384.0)
+    act(T.s2[:], T.q1[:], F.Copy, "q1", "s2", scale=-512.0)
+    ts(T.q2[:], T.q1[:], 16.0, None, A.add, None, "q1", "q2")
+    tt(T.q2[:], T.q2[:], T.q1[:], A.mult, "q1 q2", "q2")
+    act(T.s1[:], T.q2[:], F.Identity, "q2", "s1", scale=-8192.0, bias=8192.0)
+    act(T.s3[:], T.q2[:], F.Copy, "q2", "s3", scale=256.0)
+    act(T.D0G[:], T.segm[:, 0:128], F.Identity, "segm", "D0G", scale=2.0 ** 25 + 16, bias=-2.0 ** 25)
+    act(T.D0V[:], T.segm[:, 0:128], F.Identity, "segm", "D0V", scale=2.0 ** 27 + 256, bias=-2.0 ** 27)
+    ms(T.U[:, W:VOID], 0.0, "Uc+")
+    ms(T.U[:, VOID:UW], -128.0, "Uc+")
+    cp(T.prb2[:, 0:128 - NS], T.prb[:, 128:256 - NS], "prb", "prb2+")
+    ms(T.prb2[:, 128 - NS:128], 0.0, "prb2+")
     ts(T.rowA[:], m128, col(PP), NONE, A.is_gt, A.mult, "mf f2", "rowA")
     ts(T.rowB[:], m128, col(PP), NONE, A.is_equal, A.mult, "mf f2", "rowB")
+    ts(T.nI[:], m128, col(PP), -4096.0, A.is_equal, A.mult, "mf f2", "nI")
     tt(T.rowA[:], T.rowA[:], T.rowB[:], A.subtract, "rowA rowB", "rowA")
+    ts(T.If[:], m128, col(PP), None, A.is_equal, None, "mf f2", "If")
+    ts(T.nIf[:], m128, col(PP), -1.0, A.is_equal, A.mult, "mf f2", "nIf")
+    ts(T.nI16[:], m128, col(PP), -16.0, A.is_equal, A.mult, "mf f2", "nI16")
     tt(T.TNb[:], T.rowA[:], T.BLK[:], A.mult, "rowA BLK", "TNb")
-    for k in range(8):
+    ts(T.Ind[:], T.w8[:], col(PG), 256.0, A.is_equal, A.mult, "w8 f1", "Ind")
+    for k in range(4):
         ts(T.D0C[:, 256 * k:256 * k + 256], T.segm[:], 2.0 ** 20 + 1, -2.0 ** 20, A.mult, A.add, "segm", "D0C+")
-    ts(T.D0G[:], T.segm[:, 0:128], 2.0 ** 25 + 16, -2.0 ** 25, A.mult, A.add, "segm", "D0G")
-    ts(T.D0V[:], T.segm[:, 0:128], 2.0 ** 27 + 256, -2.0 ** 27, A.mult, A.add, "segm", "D0V")
     for h in range(2):
         ts(T.TH0[:, h, :], T.thb[:], 256.0, -SQ, A.mult, A.add, "thb", "TH0+")
     for t in range(4):
         ts(col(RC_ + t), col(PI), float(RHO[t]), NONE, A.is_equal, A.mult, "f0", "fr%d" % t)
+    ms(T.FE[:], 1.0, " ".join("F%d" % k for k in range(7)))
+    ms(T.FE2[:], 1.0, " ".join("E%d" % k for k in range(6)))
 
-    def fills(n, items):
+    def fills(n, rows, items):
         for f, v in items:
-            sel(T[n][0:K, :], T[n][0:K, :], BP, A.not_equal, v, -8 * f, 1, n, n)
+            sel(T[n][0:rows, :], T[n][0:rows, :], BP, A.not_equal, v, -8 * f, 1, n, n)
 
     def tn(t):
         sel(T.TN[:, 128 * t:128 * t + 128], T.TNb[:], [[0, 8], [1, 16]], A.not_equal, 0.0, -RHO[t], 0, "TNb", "TN%d" % t)
 
-    def ctg(t):
-        sel(T.sa[0:K, :], T.CTa[0:K, :], [[0, 8], [1, 16]], A.not_equal, 0.0, -RHO[t], 0, "CTa", "sa")
-        sel(T.sb[0:K, :], T.CTb[0:K, :], [[0, 8], [1, 16]], A.is_equal, 0.0, -RHO[t], 0, "CTb", "sb")
+    def ct(t):
+        n, a = "CT%d" % t, 128 * t
+        sel(T.CT[0:K2R, a:a + 128], T.CTa[0:K2R, :], [[0, 8], [1, 16]], A.not_equal, 0.0, -RHO[t], 0, "CTa", n)
+        c = T.CT[0:K2R, a + RHO[t]:a + 128:16]
+        for f, v in ((0, -16.0), (1, 1.0), (2, NONE), (5, 240.0)):
+            sel(c, c, [[-1, 8]], A.not_equal, v, -8 * f, 1, n, n)
 
-    def ctv(t):
-        tt(T.CT[0:K, 128 * t:128 * t + 128], T.sa[0:K, :], T.sb[0:K, :], A.add, "sa sb", "CT%d" % t)
-
-    sel(T.s0[0:K, :], T.s0[0:K, :], BP, A.is_equal, 0.0, -8 * 2, 1, "s0", "s0")
-    sel(T.s1[0:K, :], T.s1[0:K, :], BP, A.is_equal, 0.0, -8 * 11, 1, "s1", "s1")
-    fills("s0", [(5, -8192.0), (7, -8192.0)])
-    fills("CTa", [(10, 1.0), (9, NONE), (11, NONE)])
-    fills("CTb", [(0, -16.0), (1, 1.0), (6, NONE), (11, 240.0)])
+    sel(T.s0[0:K1R, :], T.s0[0:K1R, :], BP, A.is_equal, 0.0, 0, 1, "s0", "s0")
+    sel(T.s1[0:K1R, :], T.s1[0:K1R, :], BP, A.is_equal, 0.0, -8 * 6, 1, "s1", "s1")
+    sel(T.s2[0:K1R, :], T.s2[0:K1R, :], BP, A.is_equal, 0.0, -8, 1, "s2", "s2")
+    sel(T.s3[0:K1R, :], T.s3[0:K1R, :], BP, A.is_equal, 0.0, -8 * 6, 1, "s3", "s3")
+    fills("s0", K1R, [(2, -8192.0)])
+    fills("s2", K1R, [(3, 256.0)])
+    fills("CTa", K2R, [(4, 1.0)])
+    fills("s0", K1R, [(4, -8192.0)])
+    fills("CTa", K2R, [(2, -NONE)])
+    fills("CC", K1R, [(2, 2.0 ** 17)])
+    fills("CTa", K2R, [(3, NONE)])
+    fills("CC", K1R, [(0, 2.0 ** 17)])
+    fills("CTa", K2R, [(5, 2 * NONE)])
+    fills("CC", K1R, [(4, 2.0 ** 17)])
     tn(0)
-    ctg(0)
-    sel(T.s2[0:K, :], T.s2[0:K, :], BP, A.is_equal, 0.0, 0, 1, "s2", "s2")
-    sel(T.s3[0:K, :], T.s3[0:K, :], BP, A.is_equal, 0.0, -8 * 11, 1, "s3", "s3")
-    fills("s2", [(3, 256.0)])
-    fills("CC", [(5, 2.0 ** 17), (2, 2.0 ** 17), (7, 2.0 ** 17), (8, 1.0), (11, 201.0 * 8192)])
-    for t in range(1, 4):
-        iota(T.ri[:, 128 * t:128 * t + 128], [[1, 128]], 1 + t, 0, "ri%d" % t)
+    fills("CC", K1R, [(5, 1.0)])
+    ct(0)
+    fills("CC", K1R, [(6, 201.0 * 8192)])
 
-    ts(T.MQ[:], T.mif[:], col(PI), None, A.is_equal, None, "mif f0", "MQ")
-    ts(T.TM[:], T.mf[:], float(TR), None, A.add, None, "mf", "TM")
-    tt(T.TM[:], T.TM[:], T.MQ[:], A.mult, "TM MQ", "TM")
-    ts(col(EV), col(OD), -1.0, 1.0, A.mult, A.add, "f3", "f4")
-    ms(T.SEL[:, 0:112], 0.0, "SEL+")
-    ms(T.SEL[:, 128:240], 0.0, "SEL+")
-    ms(T.SEL[:, 112:128], 2.0 ** 24, "SEL+")
-    ms(T.FE[:], 1.0, " ".join("F%d" % k for k in range(NF)))
-    ms(T.half[:], 0.5, "half")
-    ms(T.pw2[:], 0.0, "pw2")
-    scan(T.pw[:], T.half[:], T.pw2[:], A.mult, A.add, "half pw2", "pw", 2.0)
-    ts(T.pw2[:], T.mif[:, 0:16], col(PI), None, A.is_equal, None, "mif f0", "pw2")
-    tt(T.pw[:], T.pw[:], T.pw2[:], A.mult, "pw pw2", "pw")
-    op("v", lambda: V.tensor_reduce(col(SK), T.pw[:, 0:14], AxisListType.X, A.add), "pw", "f5")
-    ts(col(BK), col(SK), 0.5, -0.5, A.mult, A.add, "f5", "f6")
-    ts(col(R14), col(PI), 14.0, None, A.is_equal, None, "f0", "f10")
-    ts(col(R15), col(PI), 15.0, None, A.is_equal, None, "f0", "f11")
-    ts(col(HB), col(PI), 14.0, 0.5, A.is_lt, A.mult, "f0", "f12")
-    tt(col(CL), col(HB), col(R14), A.subtract, "f12 f10", "f7")
-    tt(col(CR), col(HB), col(R15), A.subtract, "f12 f11", "f8")
-    ts(col(N14), col(R14), -1.0, None, A.mult, None, "f10", "f9")
-    ts(T.dm[:], T.mf[:], 1.0 / 1024, None, A.mult, None, "mf", "dm")
-    ts(T.bH[:, 0:256], T.dm[:], col(R15), col(CL), A.mult, A.add, "dm f11 f7", "bH")
-    ts(T.bH[:, 256:512], T.dm[:], col(N14), col(CR), A.mult, A.add, "dm f9 f8", "bH")
+    def late_columns():
+        ms(T.half[:], 0.5, "half")
+        ms(T.pw2[:], 0.0, "pw2")
+        ts(col(EV), col(OD), -1.0, 1.0, A.mult, A.add, "f3", "f4")
+        ts(col(R14), col(PI), 14.0, None, A.is_equal, None, "f0", "f10")
+        ts(col(R15), col(PI), 15.0, None, A.is_equal, None, "f0", "f11")
+        ts(col(HB), col(PI), 14.0, 0.5, A.is_lt, A.mult, "f0", "f12")
+        scan(T.pw[:], T.half[:], T.pw2[:], A.mult, A.add, "half pw2", "pw", 2.0)
+        act(T.dm[:], T.mf[:], F.Copy, "mf", "dm", scale=1.0 / 1024)
+        tt(col(CL), col(HB), col(R14), A.subtract, "f12 f10", "f7")
+        tt(col(CR), col(HB), col(R15), A.subtract, "f12 f11", "f8")
+        ts(T.pw2[:], T.mif[:, 0:16], col(PI), None, A.is_equal, None, "mif f0", "pw2")
+        ts(col(N14), col(R14), -1.0, None, A.mult, None, "f10", "f9")
+        tt(T.pw[:], T.pw[:], T.pw2[:], A.mult, "pw pw2", "pw")
+        op("v", lambda: V.tensor_reduce(col(SK), T.pw[:, 0:14], AxisListType.X, A.add), "pw", "f5")
+        ts(T.bH[:, 0:256], T.dm[:], col(R15), col(CL), A.mult, A.add, "dm f11 f7", "bH")
+        ts(T.bH[:, 256:512], T.dm[:], col(N14), col(CR), A.mult, A.add, "dm f9 f8", "bH")
+        ts(col(BK), col(SK), 0.5, -0.5, A.mult, A.add, "f5", "f6")
+
+    def late_tiles():
+        ts(T.MQ[:], T.mif[:], col(PI), None, A.is_equal, None, "mif f0", "MQ")
+        ts(T.TM[:], T.mf[:], float(TR), None, A.add, None, "mf", "TM")
+        ms(T.SEL[:, 0:112], 0.0, "SEL+")
+        ms(T.SEL[:, 128:240], 0.0, "SEL+")
+        ms(T.SEL[:, 112:128], 2.0 ** 24, "SEL+")
+        tt(T.TM[:], T.TM[:], T.MQ[:], A.mult, "TM MQ", "TM")
 
     def fe(f, n=1):
         return T.FE[:, :, 8 * f:8 * (f + n)]
 
-    ALLF = " ".join("F%d" % k for k in range(NF))
+    def fe2(f, n=1):
+        return T.FE2[:, :, 8 * f:8 * (f + n)]
+
+    ALLF = " ".join("F%d" % k for k in range(7)) + " I1"
+    ALLE = " ".join("E%d" % k for k in range(6)) + " I1"
     GB, VB = [T.bA, T.bB], [T.bC, T.bD]
     GN, VN = ["bA", "bB"], ["bC", "bD"]
     win = T.U[:, 0:UW]
-    FT = T.FT[0:K, :]
+    FT, FT2 = T.FT[0:K1R, :], T.FT2[0:K2R, :]
+    X0 = 4096 - 16 * NS
+
+    def gains(h, t):
+        a, b = 2048 * h, 2048 * h + 2048
+        mm(GB[h][:, 0:128], T.prb[:, 0:128] if h == 0 else T.prb2[:], T.nI[:], True, False, ("prb" if h == 0 else "prb2") + " nI", GN[h])
+        for i in range(16):
+            mm(GB[h][:, 0:128], T.Mx[:, a + i:b:16], T.I256[:], False, False, ("Mx0" if h == 0 else "Mx1 Mx2") + " I256", GN[h])
+
+    def votes(h):
+        a, b = 2048 * h, 2048 * h + 2048
+        mm(VB[h][:, 0:128], T.hib[:, 128 * h:128 * h + 128], T.If[:], True, False, "hib If", VN[h])
+        for i in range(16):
+            mm(VB[h][:, i:128:16], T.got[:, a + i:b:16], T.Ind[:], False, i == 15, "got%d Ind" % h, VN[h])
 
     for t in range(4):
         src = "T%d" % t
         for h in range(2):
             a, b = 2048 * h, 2048 * h + 2048
-            o = T.off[:, 128 * h:128 * h + 128]
-            act(T.got[:, a:b], win.indirect(o), F.Identity, "off " + UALL, "got%d" % h, scale=16.0, bias=-2048.0)
-            op("v", lambda: V.tensor_tensor(T.Mx[:, a:b], win.indirect(o), T.PX[:, a:b], A.max), "off PXs PXv " + UALL, "Mx%d" % h)
-            if h == 0:
-                ts(T.hii[:], T.z[:], 9, 255, A.arith_shift_right, A.bitwise_and, "z", "hii")
-                ts(T.Nn[:], T[src][:], NONE / 2, None, A.is_ge, None, src, "Nn")
-                ts(T.Tt[:], T[src][:], col(RC_ + t), None, A.max, None, src + " fr%d" % t, "Tt")
-                cp(T.hib[:], T.hii[:], "hii", "hib")
-            mm(GB[h][:, 0:128], T.prb[:, 128 * h:128 * h + 128], T.nI[:], True, False, "prb nI", GN[h])
-            for i in range(16):
-                mm(GB[h][:, 0:128], T.Mx[:, a + i:b:16], T.I256[:], False, False, "Mx%d I256" % h, GN[h])
-            mm(VB[h][:, 0:128], T.hib[:, 128 * h:128 * h + 128], T.I1[:], True, False, "hib I1", VN[h])
-            for i in range(16):
-                mm(VB[h][:, i:128:16], T.got[:, a + i:b:16], T.Ind[:], False, i == 15, "got%d Ind" % h, VN[h])
-        mm(T.bF[:, 0:256], T.TN[:, 128 * t:128 * t + 128], T.Nn[:], True, False, "TN%d Nn" % t, "bF")
+            act(T.got[:, a:b], win.indirect(T.off[:, 128 * h:128 * h + 128]), F.Identity, "off " + UALL, "got%d" % h, scale=16.0, bias=-2048.0)
+        op("v", lambda: V.tensor_tensor(T.Mx[:, 0:2048], win.indirect(T.off[:, 0:128]), T.PX[:, 0:2048], A.max),
+           "off PXs PXv " + UALL, "Mx0")
+        ts(T.hib[:], T.off[:], 1.0 / 32, 1024.0 - 0.484375, A.mult, A.add, "off", "hib")
+        op("v", lambda: V.tensor_tensor(T.Mx[:, 2048:X0], win.indirect(T.off[:, 128:256 - NS]), T.PX[:, 2048:X0], A.max),
+           "off PXs PXv " + UALL, "Mx1")
+        gains(0, t)
+        votes(0)
+        mm(T.bG[:], T.nI16[:], T.PX[:, X0:4096], True, False, "nI16 PXs PXv", "bG")
+        mm(T.bG[:], T.I1[:], T.got[:, X0:4096], False, True, "I1 got1", "bG")
+        votes(1)
+        act(T.Mx[:, X0:4096], T.bG[:], F.Relu, "bG", "Mx2", scale=1.0 / 16, bias=128.0)
+        gains(1, t)
+        act(T.Nn[:], T[src][:], F.Relu, src, "Nn", bias=1.0 - NONE)
+        act(T.Tt[:], T[src][:], F.Identity, src + " fr%d" % t, "Tt", bias=col(RC_ + t))
+        for h in range(4):
+            a, b = 1024 * h, 1024 * h + 1024
+            scan(T.K1[:, a:b], T.D0C[:], T.got[:, a:b], A.add, A.max, "D0C got%d" % (h // 2), "K1%d+" % (h // 2))
         for h in range(2):
-            a, b = 2048 * h, 2048 * h + 2048
-            scan(T.K1[:, a:b], T.D0C[:], T.got[:, a:b], A.add, A.max, "D0C got%d" % h, "K1%d" % h)
-        if t == 0:
-            tt(T.CP[0:K, :], T.s0[0:K, :], T.s1[0:K, :], A.add, "s0 s1", "CP")
-            tt(T.CX[0:K, :], T.s2[0:K, :], T.s3[0:K, :], A.add, "s2 s3", "CX")
-        ctv(t)
+            scan(T.VKs[:, h, :], T.D0V[:], VB[h][:, 0:128], A.add, A.max, "D0V " + VN[h], "VKs+")
         ts(T.R[:], T.K1[:, 15:4096:16], SQ - 7.5, None, A.add, None, "K10 K11", "R")
         for h in range(2):
             mm(GB[h][:, 0:128], T.K1[:, 2048 * h + 15:2048 * h + 2048:16], T.If[:], False, False, "K1%d If" % h, GN[h])
             mm(GB[h][:, 0:128], T.R[:, 128 * h:128 * h + 128], T.nIf[:], False, True, "R nIf", GN[h])
-        for h in range(2):
-            scan(T.VKs[:, h, :], T.D0V[:], VB[h][:, 0:128], A.add, A.max, "D0V " + VN[h], "VKs+")
+        mm(T.bF[:, 0:256], T.TN[:, 128 * t:128 * t + 128], T.Nn[:], True, False, "TN%d Nn" % t, "bF")
         vk = T.VKs[:, :, 15:128:16]
-        ts(T.VKi[:], vk, 2.0 ** 23, None, A.add, None, "VKs", "VKi")
-        ts(T.ns[:], vk, -2.0 ** 23, None, A.is_lt, None, "VKs", "ns")
-        ts(T.tki[:], T.VKi[:], 255, None, A.bitwise_and, None, "VKi", "tki")
-        cp(fe(10), T.tki[:], "tki", "F10")
+        ts(fe2(3), vk, -2.0 ** 23, None, A.is_lt, None, "VKs", "E3")
+        if t == 0:
+            tt(T.CP[0:K1R, :], T.s0[0:K1R, :], T.s1[0:K1R, :], A.add, "s0 s1", "CP")
+            tt(T.CX[0:K1R, :], T.s2[0:K1R, :], T.s3[0:K1R, :], A.add, "s2 s3", "CX")
         for h in range(2):
             scan(T.GKs[:, h, :], T.D0G[:], GB[h][:, 0:128], A.add, A.max, "D0G " + GN[h], "GKs+")
         gk = T.GKs[:, :, 15:128:16]
-        th = T.TH0 if t == 0 else T.TH
-        thn = "TH0" if t == 0 else "TH"
+        th, thn = (T.TH0, "TH0") if t == 0 else (T.TH, "TH")
         ts(T.GKi[:], gk, SQ, None, A.add, None, "GKs", "GKi")
-        tt(fe(6), gk, th[:], A.is_lt, "GKs " + thn, "F6")
-        tt(T.us[:], gk, th[:], A.is_ge, "GKs " + thn, "us")
-        ts(T.DEC[:, :, 0:8], T.GKi[:], 4, 15, A.arith_shift_right, A.bitwise_and, "GKi", "DEC0")
-        ts(T.DEC[:, :, 8:16], T.GKi[:], 8, 15, A.arith_shift_right, A.bitwise_and, "GKi", "DEC1")
-        ts(T.DEC[:, :, 16:24], T.GKi[:], 15, None, A.bitwise_and, None, "GKi", "DEC2")
-        tt(fe(7), fe(6), T.ns[:], A.max, "F6 ns", "F7")
-        cp(fe(0, 3), T.DEC[:], "DEC0 DEC1 DEC2", "F0 F1 F2")
-        act(fe(3, 3), fe(0, 3), F.Square, "F0 F1 F2", "F3 F4 F5", bias=-8.0)
-        tt(fe(8), fe(7), T.cnum[:], A.mult, "F7 cnum", "F8")
-        tt(fe(9), T.us[:], T.ns[:], A.max, "us ns", "F9")
+        tt(fe2(2), gk, th[:], A.is_lt, "GKs " + thn, "E2")
+        ts(T.DEC[:, :, 0:8], T.GKi[:], 15, None, A.bitwise_and, None, "GKi", "DEC0")
+        ts(T.DEC[:, :, 8:16], T.GKi[:], 4, 15, A.arith_shift_right, A.bitwise_and, "GKi", "DEC1")
+        tt(fe(4), fe2(2), fe2(3), A.max, "E2 E3", "F4")
+        cp(fe(0, 2), T.DEC[:, :, 0:16], "DEC0 DEC1", "F0 F1")
+        act(T.FE[:, 0, 40:48], T.FE[:, 0, 32:40], F.Copy, "F4 f2", "F5+", scale=col(PP))
+        act(T.FE[:, 1, 40:48], T.FE[:, 1, 32:40], F.Copy, "F4 f13", "F5+", scale=col(PH))
+        act(fe(2, 2), fe(0, 2), F.Square, "F0 F1", "F2 F3", bias=-8.0)
         for h in range(2):
-            mm(T.bE[0:K, 128 * h:128 * h + 128], T.FE[:, h, :], T.I1[:], True, True, ALLF + " I1", "bE")
-        act(FT, T.bE[0:K, 0:256], F.Copy, "bE", "FT")
-        mm(T.bG[:, 0:256], T.CP[0:K, :], FT, True, True, "CP FT", "bG")
-        mm(T.bF[:, 0:256], T.CT[0:K, 128 * t:128 * t + 128], FT, False, True, "CT%d FT" % t, "bF")
-        mm(T.bE[:, 256:512], T.CX[0:K, :], FT, True, True, "CX FT", "bE")
+            mm(T.bE[0:K1R, 128 * h:128 * h + 128], T.FE[:, h, :], T.I1[:], True, True, ALLF, "bE")
+        act(FT, T.bE[0:K1R, 0:256], F.Copy, "bE", "FT")
+        ts(T.VKi[:], vk, 2.0 ** 23 - 1024, None, A.add, None, "VKs", "VKi")
+        ts(T.DEC[:, :, 16:24], T.GKi[:], 8, 15, A.arith_shift_right, A.bitwise_and, "GKi", "DEC2")
+        ts(T.tki[:], T.VKi[:], 255, None, A.bitwise_and, None, "VKi", "tki")
+        cp(fe2(0, 2), T.DEC[:, :, 8:24], "DEC1 DEC2", "E0 E1")
+        cp(fe2(4), T.tki[:], "tki", "E4")
+        if t == 0:
+            late_columns()
+        mm(T.bG[:, 0:256], T.CP[0:K1R, :], FT, True, True, "CP FT", "bG")
+        for h in range(2):
+            mm(T.bC[0:K2R, 128 * h:128 * h + 128], T.FE2[:, h, :], T.I1[:], True, True, ALLE, "bC")
+        if t < 3:
+            for h in range(2):
+                mm(T.bC[:, 256 + 8 * h:264 + 8 * h], T.onesb[:, 0:128], T.FE2[:, h, 16:24], True, True, "onesb E2", "bC")
+        act(FT2, T.bC[0:K2R, 0:256], F.Copy, "bC", "FT2")
         tt(T.Z[:], T.bG[:, 0:256], T.ci[:], A.min, "bG ci", "Z")
-        mm(T.bG[:, 256:512], T.CC[0:K, :], FT, True, False, "CC FT", "bG")
+        mm(T.bG[:, 256:512], T.CC[0:K1R, :], FT, True, False, "CC FT", "bG")
         mm(T.bG[:, 256:512], T.BLK[:], T.Z[:], False, True, "BLK Z", "bG")
+        mm(T.bF[:, 0:256], T.CT[0:K2R, 128 * t:128 * t + 128], FT2, False, True, "CT%d FT2" % t, "bF")
+        mm(T.bE[:, 256:512], T.CX[0:K1R, :], FT, True, True, "CX FT", "bE")
+        colA = T.bG[:, 256:512]
+        ts(T.A1[:], colA, col(SK), col(BK), A.mult, A.add, "bG f5 f6", "A1")
         tt(T["Tn%d" % t][:], T.bF[:, 0:256], T.Tt[:], A.min, "bF Tt", "Tn%d" % t)
+        if t < 3:
+            act(T.junk[:], T.bC[:, 256:272], F.Copy, "bC", "junk msum", accum_out=T.msum[:, 0:1])
         act(T.Xs[:], T.bE[:, 256:512], F.Copy, "bE", "Xs")
         dst = T.cores[(rank + 1) % N] if t < 3 else T.cores[(rank - 3) % N]
         es = topo.engines(core, dst)[::2]
@@ -392,14 +443,13 @@ def rank_program(g, core, T, topo):
         wr["T%d" % (t + 1)] = ("a%d" % (t + 1), len(es))
         nloc = len(es)
         if t < 3:
+            rot(t + 1)
             tn(t + 1)
-            ctg(t + 1)
-        colA = T.bG[:, 256:512]
-        ts(T.A1[:], colA, col(SK), col(BK), A.mult, A.add, "bG f5 f6", "A1")
+            ct(t + 1)
         ts(T.A2[:], T.A1[:], 1, None, A.bitwise_and, None, "A1", "A2")
         tt(T.lhs[:], T.A2[:], T.bH[:, 0:256], A.subtract, "A2 bH", "lhs")
+        act(T.lhsE[:], T.lhs[:], F.Copy, "lhs f4", "lhsE", scale=col(EV))
         tt(T.rhs[:], T.A2[:], T.bH[:, 256:512], A.subtract, "A2 bH", "rhs")
-        ts(T.lhsE[:], T.lhs[:], col(EV), None, A.mult, None, "lhs f4", "lhsE")
         ts(T.lhsO[:], T.lhs[:], col(OD), None, A.mult, None, "lhs f3", "lhsO")
 
         def gram(bn, pos, gr, half):
@@ -419,45 +469,50 @@ def rank_program(g, core, T, topo):
             for k in range(2):
                 gram(bn, 256 * (pair % 2) + 128 * k, 2 * pair + k, 1)
             last[bn] = cnt["t"]
+        if t == 0:
+            late_tiles()
         tt(T.M1[:], colA, T.MQ[:], A.mult, "bG MQ", "M1")
         scan(T.L1[:], T.segm[:], T.M1[:], A.mult, A.add, "segm M1", "L1")
         cp(T.l1u[:], T.L1[:, 15:256:16], "L1", "l1u")
         op("v", lambda: V.tensor_tensor(T.vals[:], win.indirect(T.l1u[:]), T.Xs[:], A.min), "l1u Xs " + UALL, "vals")
         for k, bn, q in ((0, "bA", "s"), (1, "bB", "s"), (2, "bC", "v"), (3, "bD", "s"), (4, "bE", "v"), (5, "bF", "s")):
             mt = T["mt%d" % k]
+            if k == 5 and t < 3:
+                codes_x(t + 1)
             if q == "s":
                 act(mt[:], T[bn][:], F.Relu, bn, "mt%d" % k, bias=-3.5)
             else:
                 ts(mt[:], T[bn][:], -3.5, 0.0, A.add, A.max, bn, "mt%d" % k)
-        if t < 3:
-            for h in range(2):
-                mm(T.bF[:, 256 + 8 * h:264 + 8 * h], T.onesb[:, 0:128], T.FE[:, h, 48:56], True, True, "onesb F6", "bF")
-            op("v", lambda: V.tensor_reduce(T.msum[:, 0:1], T.bF[:, 256:272], AxisListType.X, A.add), "bF", "msum0")
-            cp(T.mint[:, 0:1], T.msum[:, 0:1], "msum0", "mint0")
-            ts(T.mint[:, 1:2], T.mint[:, 0:1], 255, None, A.bitwise_and, None, "mint0", "mint1")
-            ts(T.msum[:, 1:2], T.mint[:, 1:2], 256.0, None, A.mult, None, "mint1", "msum1")
-            ts(T.TH[:], T.TH0[:], T.msum[:, 1:2], None, A.add, None, "TH0 msum1", "TH")
-            rot(t + 1)
-            codes_start()
-            codes(t + 1)
         for gr in range(8):
+            if gr == 4 and t < 3:
+                codes_start()
+                codes_y(t + 1)
             mm(T.bG[:, 0:256], T.SEL[:, 112 - 16 * gr:240 - 16 * gr], T["mt%d" % (gr // 2)][:, 256 * (gr % 2):256 * (gr % 2) + 256],
                gr == 0, False, "SEL mt%d" % (gr // 2), "bG")
         for gr in range(8):
             mm(T.bG[:, 128:256], T.SEL[:, 112 - 16 * gr:240 - 16 * gr], T["mt%d" % (4 + gr // 4)][:, 128 * (gr % 4):128 * (gr % 4) + 128],
                False, gr == 7, "SEL mt%d" % (4 + gr // 4), "bG")
+        if t < 3:
+            codes(t + 1)
+            act(T.m16[:, 0:1], T.msum[:, 0:1], F.Identity, "msum", "m16", bias=49152.0 - 127.5)
+            act(T.msum[:, 1:2], T.msum[:, 0:1], F.Identity, "msum", "mb", scale=256.0, bias=256.0 * 49152)
+            act(T.msum[:, 2:3], T.m16[:, 0:1], F.Identity, "m16 mb", "mc", scale=-256.0, bias=T.msum[:, 1:2])
+            act(T.TH[:], T.TH0[:], F.Identity, "TH0 mc", "TH", bias=T.msum[:, 2:3])
         tt(T.dm[:], T.bG[:, 0:256], T.TM[:], A.min, "bG TM", "dm")
         scan(T.D1[:], T.segm[:], T.dm[:], A.mult, A.add, "segm dm", "D1")
         tt(T.l2f[:], T.L1[:, 15:256:16], T.D1[:, 15:256:16], A.max, "L1 D1", "l2f")
         cp(T.l2u[:], T.l2f[:], "l2f", "l2u")
         op("v", lambda: V.tensor_copy(win.indirect(T.l2u[:]), T.vals[:]), "l2u vals", UALL)
 
-    ts(T.yt32[:], T.T4[:], 256.0, None, A.min, None, "T4", "yt32")
-    dma("y", T.yt[:], T.yt32[:], "yt32", "yt")
     for k in range(16):
-        mm(T.bA[:], T.I1[:], T.U[:, k:W:16], k == 0, k == 15, "I1 " + UALL, "bA")
-    act(T.yc32[:], T.bA[:], F.Copy, "bA", "yc32")
-    dma("y", T.yc[:], T.yc32[:], "yc32", "yc")
+        mm(T.bA[:, 0:384], T.I1[:], T.U[:, k:6144:16], k == 0, k == 15, "I1 " + UALL, "bA")
+    for k in range(8):
+        scan(T.ysc[:, 256 * k:256 * k + 256], T.segm[:], T.U[:, 6144 + 256 * k:6400 + 256 * k], A.mult, A.add, "segm " + UALL, "ysc+")
+    cp(T.yc32[:, 384:512], T.ysc[:, 15:2048:16], "ysc", "yc1")
+    ts(T.yt32[:], T.T4[:], 256.0, None, A.min, None, "T4", "yt32")
+    act(T.yc32[:, 0:384], T.bA[:, 0:384], F.Copy, "bA", "yc0")
+    dma("s", T.yt[:], T.yt32[:], "yt32", "yt")
+    dma("y", T.yc[:], T.yc32[:], "yc0 yc1", "yc")
     fin = [(q, n) for q, n in cnt.items() if n] + [("d%d" % k, 16) for k in range(ndma[0])]
     need("g", fin)
     g.wait_ge(T.sem.loc, 4 * nloc)

@@ -17,7 +17,7 @@ def _b(name, cols, dtype, where="sbuf"):
     SCRATCH[name] = (where, [128] + (list(cols) if isinstance(cols, (list, tuple)) else [cols]), dtype)
 
 
-for _n, _c in (("U", UW), ("got", 4096), ("Mx", 4096), ("PX", 4096), ("D0C", 1024), ("D0G", 128), ("D0V", 128), ("segm", 256),
+for _n, _c in (("U", UW), ("got", 4096), ("Mx", 4096), ("PX", 4096), ("D0C", 512), ("BLKN", 128), ("D0G", 128), ("D0V", 128), ("segm", 256),
                ("T0", 256), ("T1", 256), ("T2", 256), ("T3", 256), ("T4", 256), ("Tn0", 256), ("Tn1", 256), ("Tn2", 256), ("Tn3", 256),
                ("Tt", 256), ("Nn", 256), ("prb", 256), ("prb2", 128), ("FT", 256), ("FT2", 256), ("rhs", 256), ("lhs", 256),
                ("lhsE", 256), ("lhsO", 256), ("Xs", 256), ("vals", 256), ("mt0", 512), ("mt1", 512), ("mt2", 512), ("mt3", 512),
@@ -26,17 +26,16 @@ for _n, _c in (("U", UW), ("got", 4096), ("Mx", 4096), ("PX", 4096), ("D0C", 102
                ("RT", 512), ("TNb", 128), ("TN", 512), ("CT", 512), ("FE", (2, K1R)), ("FE2", (2, K2R))):
     _b(_n, _c, "bfloat16")
 for _n, _c in (("xx", 256), ("pd", 256), ("GKs", (2, 128)), ("VKs", (2, 128)), ("TH0", (2, 8)),
-               ("TH", (2, 8)), ("Z", 256), ("M1", 256), ("L1", 256), ("dm", 256), ("D1", 256), ("l2f", 16),
+               ("TH", (2, 8)), ("TH20", (2, 8)), ("TH2", (2, 8)), ("Z", 256), ("dm", 256), ("D1", 256),
                ("BLK", 128), ("TM", 256), ("mif", 256), ("mf", 256), ("mgf", 128), ("w8", 8), ("colsf", 40), ("pw", 16), ("pw2", 16),
-               ("half", 16), ("msum", 4), ("junk", 16), ("yt32", 256), ("yc32", 512), ("ysc", 2048), ("mi2", 128), ("rowA", 128),
-               ("rowB", 128), ("q1", 128), ("q2", 128), ("s0", 128), ("s1", 128), ("s2", 128), ("s3", 128)):
+               ("half", 16), ("msum", 4), ("junk", 16), ("yt32", 256), ("yc32", 512), ("ysc", 2048), ("mi2", 128), ("q1", 128), ("q2", 128), ("s0", 128), ("s1", 128), ("s2", 128), ("s3", 128)):
     _b(_n, _c, "float32")
 for _n, _c in (("tsti", 256), ("z", 256), ("ci", 256), ("GKi", (2, 8)), ("DEC", (2, 24)), ("VKi", (2, 8)), ("tki", (2, 8)),
                ("A1", 256), ("A2", 256), ("thr", 8), ("thb", 8), ("mi", 128), ("ri", 128), ("pc", 8)):
     _b(_n, _c, "int32")
 for _n, _c in (("K1", 4096), ("R", 256), ("If", 128), ("nIf", 128), ("hib", 256)):
     _b(_n, _c, "float16")
-for _n, _c in (("off", 256), ("l1u", 16), ("l2u", 16)):
+for _n, _c in (("off", 256), ("l2u", 16)):
     _b(_n, _c, "uint16")
 for _n in "ABCDEFGH":
     _b("b" + _n, 512, "float32", "psum")
@@ -179,12 +178,12 @@ def rank_program(g, core, T, topo):
     iota(T.pc[:, 0:1], [[0, 1]], 0, 1, "pc0")
     iota(T.ri[:], [[1, 128]], 1, 0, "ri")
     iota(T.mgf[:], [[1, 8], [0, 16]], 0, 0, "mgf", **FL)
-    iota(col(PP), [[0, 1]], 0, 1, "f2", **FL)
-    iota(col(PH), [[0, 1]], 128, 1, "f13", **FL)
-    iota(T.mf[:], [[1, 256]], 0, 0, "mf", **FL)
     iota(T.mif[:], [[0, 16], [1, 16]], 0, 0, "mif", **FL)
-    iota(T.w8[:], [[1, 8]], 0, 0, "w8", **FL)
+    iota(col(PP), [[0, 1]], 0, 1, "f2", **FL)
+    iota(T.mf[:], [[1, 256]], 0, 0, "mf", **FL)
     iota(T.q1[:], [[0, 8], [-1, 16]], 7, 0, "q1", **FL)
+    iota(T.w8[:], [[1, 8]], 0, 0, "w8", **FL)
+    iota(col(PH), [[0, 1]], 128, 1, "f13", **FL)
     op("g", lambda: g.partition_broadcast(T.thb[:], T.thr[0:1, 0:8], 128), "thr", "thb")
 
     ms(T.onesb[:], 1.0, "onesb")
@@ -221,58 +220,63 @@ def rank_program(g, core, T, topo):
         src = "T%d" % t
         act(T.xx[:], T[src][:], F.Identity, src, "xx", scale=2.0, bias=1.0)
 
+    HALVES = [(h, slice(128 * h, 128 * h + 128)) for h in range(2)]
+
     def codes(t):
-        tt(T.pd[:], T.bA[:, 0:256], T.xx[:], A.mult, "bA xx", "pd")
-        ts(T.z[:], T.pd[:], col(KC + t), 2.0 ** 30, A.add, A.min, "pd fk%d" % t, "z")
-        ts(T.ci[:], T.z[:], 4, 8191 | 0x7FFF8000, A.arith_shift_right, A.bitwise_and, "z", "ci")
-        ts(T.off[:], T.ci[:], float(VOID), None, A.min, None, "ci", "off")
+        for h, c in HALVES:
+            tt(T.pd[:, c], T.bA[:, c], T.xx[:, c], A.mult, "bA xx", "pd%d" % h)
+        for h, c in HALVES:
+            ts(T.z[:, c], T.pd[:, c], col(KC + t), 2.0 ** 30, A.add, A.min, "pd%d fk%d" % (h, t), "z%d" % h)
+        for h, c in HALVES:
+            ts(T.ci[:, c], T.z[:, c], 4, 8191 | 0x7FFF8000, A.arith_shift_right, A.bitwise_and, "z%d" % h, "ci%d" % h)
+
+    def offsets():
+        for h, c in HALVES:
+            ts(T.off[:, c], T.ci[:, c], float(VOID), None, A.min, None, "ci%d" % h, "off+")
 
     codes_start()
     m128 = T.mf[:, 0:128]
+    ts(T.segm[:], T.mif[:], 0.0, None, A.is_gt, None, "mif", "segm")
+    ts(col(KC), col(PI), 16.0 * 613, None, A.mult, None, "f0", "fk0")
     ts(T.I1[:], m128, col(PP), None, A.is_equal, None, "mf f2", "I1")
-    ts(T.I256[:], m128, col(PP), 256.0, A.is_equal, A.mult, "mf f2", "I256")
-    ts(T.pd[:], T.tsti[:], 256.0, NONE, A.is_ge, A.mult, "tsti", "pd")
-    tt(T.T0[:], T.pd[:], T.tsti[:], A.max, "pd tsti", "T0")
+    ts(T.If[:], m128, col(PP), None, A.is_equal, None, "mf f2", "If")
+    ts(T.nIf[:], m128, col(PP), -1.0, A.is_equal, A.mult, "mf f2", "nIf")
+    act(T.BLKN[:], T.BLK[:], F.Copy, "BLK", "BLKN", scale=NONE)
+    for k in range(2):
+        act(T.D0C[:, 256 * k:256 * k + 256], T.segm[:], F.Identity, "segm", "D0C+", scale=2.0 ** 20 + 1, bias=-2.0 ** 20)
+    act(T.s0[:], T.q1[:], F.Copy, "q1", "s0", scale=16384.0)
+    act(T.q2[:], T.q1[:], F.Square, "q1", "q2", bias=8.0)
+    act(T.s2[:], T.q1[:], F.Copy, "q1", "s2", scale=-512.0)
+    act(T.s1[:], T.q2[:], F.Identity, "q2", "s1", scale=-8192.0, bias=8192.0 * 65)
+    ts(T.pd[:], T.tsti[:], 256.0, NONE, A.is_ge, A.mult, "tsti", "pd0 pd1")
+    tt(T.T0[:], T.pd[:], T.tsti[:], A.max, "pd0 pd1 tsti", "T0")
     codes_y(0)
     codes_x(0)
-    for t in range(4):
-        ts(col(KC + t), col(PI), 16.0 * 613, 16.0 * 77 * t, A.mult, A.add, "f0", "fk%d" % t)
-    ts(T.segm[:], T.mif[:], 0.0, None, A.is_gt, None, "mif", "segm")
+    act(T.s3[:], T.q2[:], F.Identity, "q2", "s3", scale=256.0, bias=-16384.0)
+    act(T.dm[:], T.mf[:], F.Copy, "mf", "dm", scale=1.0 / 1024)
+    act(T.I256[:], T.I1[:], F.Copy, "I1", "I256", scale=256.0)
+    act(T.nI[:], T.I1[:], F.Copy, "I1", "nI", scale=-4096.0)
     codes(0)
+    offsets()
     for i in range(16):
         if i < 6:
             act(T.PX[:, i:4096:16], T.prb[:], F.Copy, "prb", "PXs+")
         else:
             cp(T.PX[:, i:4096:16], T.prb[:], "prb", "PXv+")
-    act(T.s0[:], T.q1[:], F.Copy, "q1", "s0", scale=16384.0)
-    act(T.s2[:], T.q1[:], F.Copy, "q1", "s2", scale=-512.0)
-    ts(T.q2[:], T.q1[:], 16.0, None, A.add, None, "q1", "q2")
-    tt(T.q2[:], T.q2[:], T.q1[:], A.mult, "q1 q2", "q2")
-    act(T.s1[:], T.q2[:], F.Identity, "q2", "s1", scale=-8192.0, bias=8192.0)
-    act(T.s3[:], T.q2[:], F.Copy, "q2", "s3", scale=256.0)
+    act(T.nI16[:], T.I1[:], F.Copy, "I1", "nI16", scale=-16.0)
     act(T.D0G[:], T.segm[:, 0:128], F.Identity, "segm", "D0G", scale=2.0 ** 25 + 16, bias=-2.0 ** 25)
     act(T.D0V[:], T.segm[:, 0:128], F.Identity, "segm", "D0V", scale=2.0 ** 27 + 256, bias=-2.0 ** 27)
     ms(T.U[:, W:VOID], 0.0, "Uc+")
     ms(T.U[:, VOID:UW], -128.0, "Uc+")
     cp(T.prb2[:, 0:128 - NS], T.prb[:, 128:256 - NS], "prb", "prb2+")
     ms(T.prb2[:, 128 - NS:128], 0.0, "prb2+")
-    ts(T.rowA[:], m128, col(PP), NONE, A.is_gt, A.mult, "mf f2", "rowA")
-    ts(T.rowB[:], m128, col(PP), NONE, A.is_equal, A.mult, "mf f2", "rowB")
-    ts(T.nI[:], m128, col(PP), -4096.0, A.is_equal, A.mult, "mf f2", "nI")
-    tt(T.rowA[:], T.rowA[:], T.rowB[:], A.subtract, "rowA rowB", "rowA")
-    ts(T.If[:], m128, col(PP), None, A.is_equal, None, "mf f2", "If")
-    ts(T.nIf[:], m128, col(PP), -1.0, A.is_equal, A.mult, "mf f2", "nIf")
-    ts(T.nI16[:], m128, col(PP), -16.0, A.is_equal, A.mult, "mf f2", "nI16")
-    tt(T.TNb[:], T.rowA[:], T.BLK[:], A.mult, "rowA BLK", "TNb")
     ts(T.Ind[:], T.w8[:], col(PG), 256.0, A.is_equal, A.mult, "w8 f1", "Ind")
-    for k in range(4):
-        ts(T.D0C[:, 256 * k:256 * k + 256], T.segm[:], 2.0 ** 20 + 1, -2.0 ** 20, A.mult, A.add, "segm", "D0C+")
     for h in range(2):
         ts(T.TH0[:, h, :], T.thb[:], 256.0, -SQ, A.mult, A.add, "thb", "TH0+")
-    for t in range(4):
-        ts(col(RC_ + t), col(PI), float(RHO[t]), NONE, A.is_equal, A.mult, "f0", "fr%d" % t)
-    ms(T.FE[:], 1.0, " ".join("F%d" % k for k in range(7)))
-    ms(T.FE2[:], 1.0, " ".join("E%d" % k for k in range(6)))
+    act(T.TH20[:], T.TH0[:], F.Identity, "TH0", "TH20", bias=SQ)
+    ts(col(RC_), col(PI), float(RHO[0]), NONE, A.is_equal, A.mult, "f0", "fr0")
+    ms(T.FE[:, :, 48:56], 1.0, "F6")
+    ms(T.FE2[:, :, 40:48], 1.0, "E5")
 
     def fills(n, rows, items):
         for f, v in items:
@@ -302,6 +306,8 @@ def rank_program(g, core, T, topo):
     fills("CC", K1R, [(0, 2.0 ** 17)])
     fills("CTa", K2R, [(5, 2 * NONE)])
     fills("CC", K1R, [(4, 2.0 ** 17)])
+    sel(T.TNb[:], T.BLKN[:], [[1, 128]], A.is_gt, 0.0, 0, -1, "BLKN", "TNb")
+    sel(T.TNb[:], T.TNb[:], [[1, 128]], A.not_equal, -NONE, 0, -1, "TNb", "TNb")
     tn(0)
     fills("CC", K1R, [(5, 1.0)])
     ct(0)
@@ -310,12 +316,10 @@ def rank_program(g, core, T, topo):
     def late_columns():
         ms(T.half[:], 0.5, "half")
         ms(T.pw2[:], 0.0, "pw2")
-        ts(col(EV), col(OD), -1.0, 1.0, A.mult, A.add, "f3", "f4")
         ts(col(R14), col(PI), 14.0, None, A.is_equal, None, "f0", "f10")
         ts(col(R15), col(PI), 15.0, None, A.is_equal, None, "f0", "f11")
         ts(col(HB), col(PI), 14.0, 0.5, A.is_lt, A.mult, "f0", "f12")
         scan(T.pw[:], T.half[:], T.pw2[:], A.mult, A.add, "half pw2", "pw", 2.0)
-        act(T.dm[:], T.mf[:], F.Copy, "mf", "dm", scale=1.0 / 1024)
         tt(col(CL), col(HB), col(R14), A.subtract, "f12 f10", "f7")
         tt(col(CR), col(HB), col(R15), A.subtract, "f12 f11", "f8")
         ts(T.pw2[:], T.mif[:, 0:16], col(PI), None, A.is_equal, None, "mif f0", "pw2")
@@ -327,12 +331,17 @@ def rank_program(g, core, T, topo):
         ts(col(BK), col(SK), 0.5, -0.5, A.mult, A.add, "f5", "f6")
 
     def late_tiles():
+        for k in range(1, 4):
+            ts(col(KC + k), col(PI), 16.0 * 613, 16.0 * 77 * k, A.mult, A.add, "f0", "fk%d" % k)
+            ts(col(RC_ + k), col(PI), float(RHO[k]), NONE, A.is_equal, A.mult, "f0", "fr%d" % k)
         ts(T.MQ[:], T.mif[:], col(PI), None, A.is_equal, None, "mif f0", "MQ")
         ts(T.TM[:], T.mf[:], float(TR), None, A.add, None, "mf", "TM")
         ms(T.SEL[:, 0:112], 0.0, "SEL+")
         ms(T.SEL[:, 128:240], 0.0, "SEL+")
         ms(T.SEL[:, 112:128], 2.0 ** 24, "SEL+")
         tt(T.TM[:], T.TM[:], T.MQ[:], A.mult, "TM MQ", "TM")
+
+    late_columns()
 
     def fe(f, n=1):
         return T.FE[:, :, 8 * f:8 * (f + n)]
@@ -358,13 +367,16 @@ def rank_program(g, core, T, topo):
         a, b = 2048 * h, 2048 * h + 2048
         mm(VB[h][:, 0:128], T.hib[:, 128 * h:128 * h + 128], T.If[:], True, False, "hib If", VN[h])
         for i in range(16):
-            mm(VB[h][:, i:128:16], T.got[:, a + i:b:16], T.Ind[:], False, i == 15, "got%d Ind" % h, VN[h])
+            mm(VB[h][:, i:128:16], T.got[:, a + i:b:16], T.Ind[:], False, i == 15, ("got0" if h == 0 else "got1 got2") + " Ind", VN[h])
 
     for t in range(4):
         src = "T%d" % t
-        for h in range(2):
-            a, b = 2048 * h, 2048 * h + 2048
-            act(T.got[:, a:b], win.indirect(T.off[:, 128 * h:128 * h + 128]), F.Identity, "off " + UALL, "got%d" % h, scale=16.0, bias=-2048.0)
+        for k, a, b in ((2, X0, 4096), (0, 0, 2048), (1, 2048, X0)):
+            act(T.got[:, a:b], win.indirect(T.off[:, a // 16:b // 16]), F.Identity, "off " + UALL, "got%d" % k, scale=16.0, bias=-2048.0)
+            if k == 0:
+                mm(T.bG[:], T.nI16[:], T.PX[:, X0:4096], True, False, "nI16 PXs PXv", "bG")
+                mm(T.bG[:], T.I1[:], T.got[:, X0:4096], False, True, "I1 got2", "bG")
+                act(T.Mx[:, X0:4096], T.bG[:], F.Relu, "bG", "Mx2", scale=1.0 / 16, bias=128.0)
         op("v", lambda: V.tensor_tensor(T.Mx[:, 0:2048], win.indirect(T.off[:, 0:128]), T.PX[:, 0:2048], A.max),
            "off PXs PXv " + UALL, "Mx0")
         ts(T.hib[:], T.off[:], 1.0 / 32, 1024.0 - 0.484375, A.mult, A.add, "off", "hib")
@@ -372,65 +384,75 @@ def rank_program(g, core, T, topo):
            "off PXs PXv " + UALL, "Mx1")
         gains(0, t)
         votes(0)
-        mm(T.bG[:], T.nI16[:], T.PX[:, X0:4096], True, False, "nI16 PXs PXv", "bG")
-        mm(T.bG[:], T.I1[:], T.got[:, X0:4096], False, True, "I1 got1", "bG")
-        votes(1)
-        act(T.Mx[:, X0:4096], T.bG[:], F.Relu, "bG", "Mx2", scale=1.0 / 16, bias=128.0)
         gains(1, t)
+        votes(1)
         act(T.Nn[:], T[src][:], F.Relu, src, "Nn", bias=1.0 - NONE)
         act(T.Tt[:], T[src][:], F.Identity, src + " fr%d" % t, "Tt", bias=col(RC_ + t))
-        for h in range(4):
-            a, b = 1024 * h, 1024 * h + 1024
-            scan(T.K1[:, a:b], T.D0C[:], T.got[:, a:b], A.add, A.max, "D0C got%d" % (h // 2), "K1%d+" % (h // 2))
-        for h in range(2):
-            scan(T.VKs[:, h, :], T.D0V[:], VB[h][:, 0:128], A.add, A.max, "D0V " + VN[h], "VKs+")
-        ts(T.R[:], T.K1[:, 15:4096:16], SQ - 7.5, None, A.add, None, "K10 K11", "R")
-        for h in range(2):
-            mm(GB[h][:, 0:128], T.K1[:, 2048 * h + 15:2048 * h + 2048:16], T.If[:], False, False, "K1%d If" % h, GN[h])
-            mm(GB[h][:, 0:128], T.R[:, 128 * h:128 * h + 128], T.nIf[:], False, True, "R nIf", GN[h])
-        mm(T.bF[:, 0:256], T.TN[:, 128 * t:128 * t + 128], T.Nn[:], True, False, "TN%d Nn" % t, "bF")
-        vk = T.VKs[:, :, 15:128:16]
-        ts(fe2(3), vk, -2.0 ** 23, None, A.is_lt, None, "VKs", "E3")
-        if t == 0:
-            tt(T.CP[0:K1R, :], T.s0[0:K1R, :], T.s1[0:K1R, :], A.add, "s0 s1", "CP")
-            tt(T.CX[0:K1R, :], T.s2[0:K1R, :], T.s3[0:K1R, :], A.add, "s2 s3", "CX")
-        for h in range(2):
+        def payload(h):
+            c = slice(2048 * h + 15, 2048 * h + 2048, 16)
+            ts(T.R[:, 128 * h:128 * h + 128], T.K1[:, c], SQ - 7.5, SQ - 2288.0, A.add, A.max, "K1%d" % h, "R%d" % h)
+            mm(GB[h][:, 0:128], T.K1[:, c], T.If[:], False, False, "K1%d If" % h, GN[h])
+            mm(GB[h][:, 0:128], T.R[:, 128 * h:128 * h + 128], T.nIf[:], False, True, "R%d nIf" % h, GN[h])
+
+        def best(h):
             scan(T.GKs[:, h, :], T.D0G[:], GB[h][:, 0:128], A.add, A.max, "D0G " + GN[h], "GKs+")
+
+        for h in (0, 1, 2, 3, 7, 4, 5, 6):
+            a, b = 512 * h, 512 * h + 512
+            scan(T.K1[:, a:b], T.D0C[:], T.got[:, a:b], A.add, A.max, "D0C got%d" % (2 if h == 7 else h // 4), "K1%d+" % (h // 4))
+            if h == 7:
+                payload(0)
+        best(0)
+        payload(1)
+        mm(T.bF[:, 0:256], T.TN[:, 128 * t:128 * t + 128], T.Nn[:], True, False, "TN%d Nn" % t, "bF")
+        best(1)
         gk = T.GKs[:, :, 15:128:16]
         th, thn = (T.TH0, "TH0") if t == 0 else (T.TH, "TH")
-        ts(T.GKi[:], gk, SQ, None, A.add, None, "GKs", "GKi")
-        tt(fe2(2), gk, th[:], A.is_lt, "GKs " + thn, "E2")
+        th2, thn2 = (T.TH20, "TH20") if t == 0 else (T.TH2, "TH2")
+        ts(T.GKi[:], gk, SQ, 240.0, A.add, A.max, "GKs", "GKi")
+        tt(fe(4), gk, th[:], A.is_lt, "GKs " + thn, "F4")
         ts(T.DEC[:, :, 0:8], T.GKi[:], 15, None, A.bitwise_and, None, "GKi", "DEC0")
         ts(T.DEC[:, :, 8:16], T.GKi[:], 4, 15, A.arith_shift_right, A.bitwise_and, "GKi", "DEC1")
-        tt(fe(4), fe2(2), fe2(3), A.max, "E2 E3", "F4")
         cp(fe(0, 2), T.DEC[:, :, 0:16], "DEC0 DEC1", "F0 F1")
         act(T.FE[:, 0, 40:48], T.FE[:, 0, 32:40], F.Copy, "F4 f2", "F5+", scale=col(PP))
         act(T.FE[:, 1, 40:48], T.FE[:, 1, 32:40], F.Copy, "F4 f13", "F5+", scale=col(PH))
         act(fe(2, 2), fe(0, 2), F.Square, "F0 F1", "F2 F3", bias=-8.0)
+        mm(T.bE[0:K1R, 0:128], T.FE[:, 0, :], T.I1[:], True, True, ALLF, "bE")
+        mm(T.bB[0:K1R, 0:128], T.FE[:, 1, :], T.I1[:], True, True, ALLF, "bB")
+        act(T.FT[0:K1R, 0:128], T.bE[0:K1R, 0:128], F.Copy, "bE", "FTa")
         for h in range(2):
-            mm(T.bE[0:K1R, 128 * h:128 * h + 128], T.FE[:, h, :], T.I1[:], True, True, ALLF, "bE")
-        act(FT, T.bE[0:K1R, 0:256], F.Copy, "bE", "FT")
+            scan(T.VKs[:, h, :], T.D0V[:], VB[h][:, 0:128], A.add, A.max, "D0V " + VN[h], "VKs+")
+        vk = T.VKs[:, :, 15:128:16]
+        cp(T.FT[0:K1R, 128:256], T.bB[0:K1R, 0:128], "bB", "FTb")
+        if t == 0:
+            tt(T.CP[0:K1R, :], T.s0[0:K1R, :], T.s1[0:K1R, :], A.add, "s0 s1", "CP")
+            tt(T.CX[0:K1R, :], T.s2[0:K1R, :], T.s3[0:K1R, :], A.add, "s2 s3", "CX")
+        tt(fe2(2), T.GKi[:], th2[:], A.is_lt, "GKi " + thn2, "E2")
+        ts(fe2(3), vk, -2.0 ** 23, None, A.is_lt, None, "VKs", "E3")
         ts(T.VKi[:], vk, 2.0 ** 23 - 1024, None, A.add, None, "VKs", "VKi")
         ts(T.DEC[:, :, 16:24], T.GKi[:], 8, 15, A.arith_shift_right, A.bitwise_and, "GKi", "DEC2")
         ts(T.tki[:], T.VKi[:], 255, None, A.bitwise_and, None, "VKi", "tki")
         cp(fe2(0, 2), T.DEC[:, :, 8:24], "DEC1 DEC2", "E0 E1")
         cp(fe2(4), T.tki[:], "tki", "E4")
-        if t == 0:
-            late_columns()
-        mm(T.bG[:, 0:256], T.CP[0:K1R, :], FT, True, True, "CP FT", "bG")
+        mm(T.bA[:, 0:256], T.CP[0:K1R, :], FT, True, True, "CP FTa FTb", "bA")
+        colA = [(T.bG[:, 256:384], "bG"), (T.bD[:, 0:128], "bD")]
+        for h, c in HALVES:
+            mm(colA[h][0], T.CC[0:K1R, :], T.FT[0:K1R, c], True, False, "CC FT" + "ab"[h], colA[h][1])
         for h in range(2):
             mm(T.bC[0:K2R, 128 * h:128 * h + 128], T.FE2[:, h, :], T.I1[:], True, True, ALLE, "bC")
         if t < 3:
             for h in range(2):
                 mm(T.bC[:, 256 + 8 * h:264 + 8 * h], T.onesb[:, 0:128], T.FE2[:, h, 16:24], True, True, "onesb E2", "bC")
         act(FT2, T.bC[0:K2R, 0:256], F.Copy, "bC", "FT2")
-        tt(T.Z[:], T.bG[:, 0:256], T.ci[:], A.min, "bG ci", "Z")
-        mm(T.bG[:, 256:512], T.CC[0:K1R, :], FT, True, False, "CC FT", "bG")
-        mm(T.bG[:, 256:512], T.BLK[:], T.Z[:], False, True, "BLK Z", "bG")
+        for h, c in HALVES:
+            tt(T.Z[:, c], T.bA[:, c], T.ci[:, c], A.min, "bA ci%d" % h, "Z%d" % h)
+            mm(colA[h][0], T.BLK[:], T.Z[:, c], False, True, "BLK Z%d" % h, colA[h][1])
         mm(T.bF[:, 0:256], T.CT[0:K2R, 128 * t:128 * t + 128], FT2, False, True, "CT%d FT2" % t, "bF")
-        mm(T.bE[:, 256:512], T.CX[0:K1R, :], FT, True, True, "CX FT", "bE")
-        colA = T.bG[:, 256:512]
-        ts(T.A1[:], colA, col(SK), col(BK), A.mult, A.add, "bG f5 f6", "A1")
+        mm(T.bE[:, 256:512], T.CX[0:K1R, :], FT, True, True, "CX FTa FTb", "bE")
+        for h, c in HALVES:
+            ts(T.A1[:, c], colA[h][0], col(SK), col(BK), A.mult, A.add, colA[h][1] + " f5 f6", "A1%d" % h)
+        mm(T.bG[:, 0:256], T.CC[0:K1R, :], FT, True, False, "CC FTa FTb", "bG")
+        mm(T.bG[:, 0:256], T.BLK[:], T.Z[:], False, False, "BLK Z0 Z1", "bG")
         tt(T["Tn%d" % t][:], T.bF[:, 0:256], T.Tt[:], A.min, "bF Tt", "Tn%d" % t)
         if t < 3:
             act(T.junk[:], T.bC[:, 256:272], F.Copy, "bC", "junk msum", accum_out=T.msum[:, 0:1])
@@ -446,22 +468,21 @@ def rank_program(g, core, T, topo):
             rot(t + 1)
             tn(t + 1)
             ct(t + 1)
-        ts(T.A2[:], T.A1[:], 1, None, A.bitwise_and, None, "A1", "A2")
-        tt(T.lhs[:], T.A2[:], T.bH[:, 0:256], A.subtract, "A2 bH", "lhs")
-        act(T.lhsE[:], T.lhs[:], F.Copy, "lhs f4", "lhsE", scale=col(EV))
-        tt(T.rhs[:], T.A2[:], T.bH[:, 256:512], A.subtract, "A2 bH", "rhs")
+        for h, c in HALVES:
+            ts(T.A2[:, c], T.A1[:, c], 1, None, A.bitwise_and, None, "A1%d" % h, "A2%d" % h)
+        for h, c in HALVES:
+            tt(T.lhs[:, c], T.A2[:, c], T.bH[:, c], A.subtract, "A2%d bH" % h, "lhs+")
+        tt(T.rhs[:], T.A2[:], T.bH[:, 256:512], A.subtract, "A20 A21 bH", "rhs")
         ts(T.lhsO[:], T.lhs[:], col(OD), None, A.mult, None, "lhs f3", "lhsO")
 
         def gram(bn, pos, gr, half):
             ba = 32 * (gr // 2)
-            l = T.lhsE if gr % 2 == 0 else T.lhsO
-            ln = "lhsE" if gr % 2 == 0 else "lhsO"
+            l, ln, k = (T.lhs, "lhs", 16) if gr % 2 == 0 else (T.lhsO, "lhsO", 32)
             n, c0 = (256, 0) if half == 0 else (128, 128)
-            mm(T[bn][:, pos:pos + n], l[ba:ba + 32, c0:c0 + 128], T.rhs[ba:ba + 32, c0:256], True, True, ln + " rhs", bn)
+            mm(T[bn][:, pos:pos + n], l[ba:ba + k, c0:c0 + 128], T.rhs[ba:ba + k, c0:256], True, True, ln + " rhs", bn)
 
-        for k, bn in enumerate(("bA", "bB", "bC", "bD")):
-            gram(bn, 0, 2 * k, 0)
-            gram(bn, 256, 2 * k + 1, 0)
+        for gr in (0, 2, 1, 3, 4, 5, 6, 7):
+            gram("b" + "ABCD"[gr // 2], 256 * (gr % 2), gr, 0)
         last = {}
         for bn, pair in (("bE", 0), ("bF", 2), ("bE", 1), ("bF", 3)):
             if bn in last:
@@ -471,11 +492,7 @@ def rank_program(g, core, T, topo):
             last[bn] = cnt["t"]
         if t == 0:
             late_tiles()
-        tt(T.M1[:], colA, T.MQ[:], A.mult, "bG MQ", "M1")
-        scan(T.L1[:], T.segm[:], T.M1[:], A.mult, A.add, "segm M1", "L1")
-        cp(T.l1u[:], T.L1[:, 15:256:16], "L1", "l1u")
-        op("v", lambda: V.tensor_tensor(T.vals[:], win.indirect(T.l1u[:]), T.Xs[:], A.min), "l1u Xs " + UALL, "vals")
-        for k, bn, q in ((0, "bA", "s"), (1, "bB", "s"), (2, "bC", "v"), (3, "bD", "s"), (4, "bE", "v"), (5, "bF", "s")):
+        for k, bn, q in ((0, "bA", "v"), (1, "bB", "s"), (2, "bC", "v"), (3, "bD", "s"), (4, "bE", "v"), (5, "bF", "s")):
             mt = T["mt%d" % k]
             if k == 5 and t < 3:
                 codes_x(t + 1)
@@ -488,7 +505,7 @@ def rank_program(g, core, T, topo):
                 codes_start()
                 codes_y(t + 1)
             mm(T.bG[:, 0:256], T.SEL[:, 112 - 16 * gr:240 - 16 * gr], T["mt%d" % (gr // 2)][:, 256 * (gr % 2):256 * (gr % 2) + 256],
-               gr == 0, False, "SEL mt%d" % (gr // 2), "bG")
+               False, False, "SEL mt%d" % (gr // 2), "bG")
         for gr in range(8):
             mm(T.bG[:, 128:256], T.SEL[:, 112 - 16 * gr:240 - 16 * gr], T["mt%d" % (4 + gr // 4)][:, 128 * (gr % 4):128 * (gr % 4) + 128],
                False, gr == 7, "SEL mt%d" % (4 + gr // 4), "bG")
@@ -498,10 +515,16 @@ def rank_program(g, core, T, topo):
             act(T.msum[:, 1:2], T.msum[:, 0:1], F.Identity, "msum", "mb", scale=256.0, bias=256.0 * 49152)
             act(T.msum[:, 2:3], T.m16[:, 0:1], F.Identity, "m16 mb", "mc", scale=-256.0, bias=T.msum[:, 1:2])
             act(T.TH[:], T.TH0[:], F.Identity, "TH0 mc", "TH", bias=T.msum[:, 2:3])
-        tt(T.dm[:], T.bG[:, 0:256], T.TM[:], A.min, "bG TM", "dm")
-        scan(T.D1[:], T.segm[:], T.dm[:], A.mult, A.add, "segm dm", "D1")
-        tt(T.l2f[:], T.L1[:, 15:256:16], T.D1[:, 15:256:16], A.max, "L1 D1", "l2f")
-        cp(T.l2u[:], T.l2f[:], "l2f", "l2u")
+            act(T.TH2[:], T.TH20[:], F.Identity, "TH20 mc", "TH2", bias=T.msum[:, 2:3])
+        for h, c in HALVES:
+            tt(T.dm[:, c], T.bG[:, c], T.TM[:, c], A.min, "bG TM", "dm%d" % h)
+        if t < 3:
+            offsets()
+        for h, c in HALVES:
+            scan(T.D1[:, c], T.segm[:, c], T.dm[:, c], A.mult, A.add, "segm dm%d" % h, "D1%d" % h)
+        for h in range(2):
+            cp(T.l2u[:, 8 * h:8 * h + 8], T.D1[:, 128 * h + 15:128 * h + 128:16], "D1%d" % h, "l2u+")
+        op("v", lambda: V.tensor_tensor(T.vals[:], win.indirect(T.l2u[:]), T.Xs[:], A.min), "l2u Xs " + UALL, "vals")
         op("v", lambda: V.tensor_copy(win.indirect(T.l2u[:]), T.vals[:]), "l2u vals", UALL)
 
     for k in range(16):

from concourse.mybir import AluOpType as A, AxisListType, ActivationFunctionType as F

NONE = 2.0 ** 19
W = 8192
TR = 8192
VOID = 8448
UW = 8464
SQ = 20480.0
NS = 32
K1R, K2R = 56, 48
RHO = [0, 5, 10, 15]

SCRATCH = {}


def _b(name, cols, dtype, where="sbuf"):
    SCRATCH[name] = (where, [128] + (list(cols) if isinstance(cols, (list, tuple)) else [cols]), dtype)


for _n, _c in (("U", UW), ("got", 4096), ("Mx", 4096), ("PX", 4096), ("D0C", 512), ("BLKN", 128), ("D0G", 128), ("D0V", 128), ("segm", 256),
               ("T0", 256), ("T1", 256), ("T2", 256), ("T3", 256), ("T4", 256), ("Tn0", 256), ("Tn1", 256), ("Tn2", 256), ("Tn3", 256),
               ("Tt", 256), ("Nn", 256), ("prb", 256), ("prb2", 128), ("FT", 256), ("FT2", 256), ("rhs", 256), ("lhs", 256),
               ("lhsE", 256), ("lhsO", 256), ("Xs", 256), ("vals", 256), ("mt0", 512), ("mt1", 512), ("mt2", 512), ("mt3", 512),
               ("mt4", 512), ("mt5", 512), ("onesb", 256), ("I1", 128), ("I256", 128), ("nI", 128), ("nI16", 128), ("Ind", 8), ("MQ", 256),
               ("SEL", 240), ("CC", 128), ("CTa", 128), ("CP", 128), ("CX", 128), ("zb", 128), ("m16", 4),
               ("RT", 512), ("TNb", 128), ("TN", 512), ("CT", 512), ("FE", (2, K1R)), ("FE2", (2, K2R))):
    _b(_n, _c, "bfloat16")
for _n, _c in (("xx", 256), ("pd", 256), ("GKs", (2, 128)), ("VKs", (2, 128)), ("TH0", (2, 8)),
               ("TH", (2, 8)), ("TH20", (2, 8)), ("TH2", (2, 8)), ("Z", 256), ("dm", 256), ("D1", 256),
               ("BLK", 128), ("TM", 256), ("mif", 256), ("mf", 256), ("mgf", 128), ("w8", 8), ("colsf", 40), ("pw", 16), ("pw2", 16),
               ("half", 16), ("msum", 4), ("junk", 16), ("yt32", 256), ("yc32", 512), ("ysc", 2048), ("mi2", 128), ("q1", 128), ("q2", 128), ("s0", 128), ("s1", 128), ("s2", 128), ("s3", 128)):
    _b(_n, _c, "float32")
for _n, _c in (("tsti", 256), ("z", 256), ("ci", 256), ("GKi", (2, 8)), ("DEC", (2, 24)), ("VKi", (2, 8)), ("tki", (2, 8)),
               ("A1", 256), ("A2", 256), ("thr", 8), ("thb", 8), ("mi", 128), ("ri", 128), ("pc", 8)):
    _b(_n, _c, "int32")
for _n, _c in (("K1", 4096), ("R", 256), ("If", 128), ("nIf", 128), ("hib", 256)):
    _b(_n, _c, "float16")
for _n, _c in (("off", 256), ("l2u", 16)):
    _b(_n, _c, "uint16")
for _n in "ABCDEFGH":
    _b("b" + _n, 512, "float32", "psum")

SEMAPHORES = ["cv", "cs", "ct", "cg", "loc"] + ["d%d" % k for k in range(10)] + ["a%d" % k for k in range(1, 5)]


def rank_program(g, core, T, topo):
    rank = T.rank_of(core)
    if rank is None:
        return
    N = len(T.cores)
    eng = {"v": g.vector, "s": g.scalar, "t": g.tensor, "g": g, "y": g.sync}
    cnt = {"v": 0, "s": 0, "t": 0, "g": 0}
    known = {q: {} for q in eng}
    clk = {}
    wr, rd, bank = {}, {}, {}
    ndma = [0]

    def sem_of(e):
        return T.sem["c" + e] if e in cnt else T.sem[e]

    def need(q, deps):
        best = {}
        for e, n in deps:
            if known[q].get(e, 0) < n and best.get(e, 0) < n:
                best[e] = n
        for e in list(best):
            for e2 in list(best):
                if e2 != e and e in best and e2 in best and clk.get((e2, best[e2]), {}).get(e, 0) >= best[e]:
                    del best[e]
        for e, n in best.items():
            eng[q].wait_ge(sem_of(e), n)
            for k, v in clk.get((e, n), {}).items():
                if known[q].get(k, 0) < v:
                    known[q][k] = v
            known[q][e] = n

    def deps_of(q, reads, writes):
        deps = []
        for t in list(reads) + list(writes):
            if t[0] == "b":
                for e, n in bank.get(t, {}).items():
                    if e != q:
                        deps.append((e, n))
        for t in reads:
            w = wr.get(t)
            if w is not None and not (t[0] == "b" and w[0] != q):
                deps.append(w)
        for t in writes:
            if t[0] != "b":
                w = wr.get(t.rstrip("+"))
                if w is not None and not (t[-1] == "+" and w[0] == q):
                    deps.append(w)
                deps.extend(rd.get(t.rstrip("+"), {}).items())
        return deps

    def note(q, e, n, reads, writes):
        c = dict(known[q])
        c[e] = n
        clk[(e, n)] = c
        for t in reads:
            if t[0] == "b":
                bank.setdefault(t, {})[e] = n
            else:
                rd.setdefault(t, {})[e] = n
        for t in writes:
            t = t.rstrip("+")
            if t[0] == "b":
                bank.setdefault(t, {})[e] = n
            else:
                rd[t] = {}
            wr[t] = (e, n)

    def op(q, fn, reads, writes):
        reads = reads.split()
        writes = writes.split()
        need(q, deps_of(q, reads, writes))
        ins = fn()
        cnt[q] += 1
        ins.then_inc(T.sem["c" + q], 1)
        note(q, q, cnt[q], reads, writes)

    def dma(q, out, in_, reads, writes):
        reads = reads.split()
        writes = writes.split()
        need(q, deps_of("dma", reads, writes))
        name = "d%d" % ndma[0]
        ndma[0] += 1
        eng[q].dma_start(out, in_).then_inc(T.sem[name], 16)
        note(q, name, 16, reads, writes)

    V, S, P = g.vector, g.scalar, g.tensor

    def ts(out, in0, s1, s2, op0, op1, r, w):
        if op1 is None:
            op("v", lambda: V.tensor_scalar(out, in0, s1, None, op0), r, w)
        else:
            op("v", lambda: V.tensor_scalar(out, in0, s1, s2, op0, op1), r, w)

    def tt(out, a, b, o, r, w):
        op("v", lambda: V.tensor_tensor(out, a, b, o), r, w)

    def cp(out, in_, r, w):
        op("v", lambda: V.tensor_copy(out, in_), r, w)

    def scan(out, d0, d1, o0, o1, r, w, init=0.0):
        op("v", lambda: V.tensor_tensor_scan(out, d0, d1, init, o0, o1), r, w)

    def act(out, in_, func, r, w, **k):
        op("s", lambda: S.activation(out, in_, func, **k), r, w)

    def mm(out, l, x, st, sp, r, w):
        op("t", lambda: P.matmul(out, l, x, st, sp), r, w)

    def ms(ap, c, w):
        op("v", lambda: V.memset(ap, c), "", w)

    def sel(out, in_, pat, cmp, fill, base, cm, r, w):
        op("g", lambda: g.affine_select(out, in_, pat, cmp, fill, base, cm), r, w)

    dma("y", T.tsti[:], T.tst[:], "", "tsti")
    dma("s", T.prb[:], T.pr[:], "", "prb")
    dma("y", T.thr[0:1, 0:8], T.th[:], "", "thr")
    dma("y", T.U[:, 0:4096], T.cov[:, 0:4096], "", "Ua")
    dma("s", T.U[:, 4096:W], T.cov[:, 4096:W], "", "Ub")
    UALL = "Ua Ub Uc"

    PI, PG, PP, OD, EV, SK, BK, CL, CR, N14, R14, R15, HB, PH = range(14)
    KC, RC_ = 16, 20
    BP = [[-1, 8], [0, 16]]
    FL = {"allow_small_or_imprecise_dtypes": True}

    def col(k):
        return T.colsf[:, k:k + 1]

    def iota(out, pat, base, cm, w, **k):
        op("g", lambda: g.iota(out, pat, base, cm, **k), "", w)

    iota(T.pc[:, 0:1], [[0, 1]], 0, 1, "pc0")
    iota(T.ri[:], [[1, 128]], 1, 0, "ri")
    iota(T.mgf[:], [[1, 8], [0, 16]], 0, 0, "mgf", **FL)
    iota(T.mif[:], [[0, 16], [1, 16]], 0, 0, "mif", **FL)
    iota(col(PP), [[0, 1]], 0, 1, "f2", **FL)
    iota(T.mf[:], [[1, 256]], 0, 0, "mf", **FL)
    iota(T.q1[:], [[0, 8], [-1, 16]], 7, 0, "q1", **FL)
    iota(T.w8[:], [[1, 8]], 0, 0, "w8", **FL)
    iota(col(PH), [[0, 1]], 128, 1, "f13", **FL)
    op("g", lambda: g.partition_broadcast(T.thb[:], T.thr[0:1, 0:8], 128), "thr", "thb")

    ms(T.onesb[:], 1.0, "onesb")
    ms(T.zb[:], 0.0, "zb")
    ms(T.CTa[:], 0.0, "CTa")
    ms(T.CC[:], 0.0, "CC")
    ts(T.pc[:, 1:2], T.pc[:, 0:1], 15, None, A.bitwise_and, None, "pc0", "pc1")
    ts(T.pc[:, 2:3], T.pc[:, 0:1], 4, None, A.arith_shift_right, None, "pc0", "pc2")
    ts(T.pc[:, 3:4], T.pc[:, 0:1], 4, 1, A.arith_shift_right, A.bitwise_and, "pc0", "pc3")
    cp(col(PI), T.pc[:, 1:2], "pc1", "f0")
    cp(col(PG), T.pc[:, 2:3], "pc2", "f1")
    cp(col(OD), T.pc[:, 3:4], "pc3", "f3")
    ts(T.BLK[:], T.mgf[:], col(PG), None, A.is_equal, None, "mgf f1", "BLK")
    ts(T.mi[:], T.ri[:], 15, None, A.bitwise_and, None, "ri", "mi")
    ts(T.mi2[:], T.mi[:], col(PI), 2.0, A.is_equal, A.mult, "mi f0", "mi2")
    tt(T.RT[:, 0:128], T.mi2[:], T.BLK[:], A.mult, "mi2 BLK", "RT0")

    def rot(t):
        s, n = 1 + t, "RT%d" % t
        b = T.RT[:, 128 * t:128 * t + 128]
        sel(b, T.zb[:], [[-16, 8], [-1, 16]], A.not_equal, 2.0, -s, 1, "zb", n)
        sel(b, b, [[-16, 8], [-1, 16]], A.not_equal, 2.0, 16 - s, 1, n, n)
        sel(b, b, [[-16, 8], [0, 16]], A.is_ge, 0.0, 0, 1, n, n)
        sel(b, b, [[16, 8], [0, 16]], A.is_ge, 0.0, 15, -1, n, n)

    def codes_start():
        mm(T.bA[:, 0:256], T.onesb[0:1, 0:128], T.onesb[0:1, 0:256], True, False, "onesb", "bA")

    def codes_y(t):
        src = "T%d" % t
        mm(T.bA[:, 0:256], T.RT[:, 128 * t:128 * t + 128], T[src][:], False, True, "RT%d %s" % (t, src), "bA")

    def codes_x(t):
        src = "T%d" % t
        act(T.xx[:], T[src][:], F.Identity, src, "xx", scale=2.0, bias=1.0)

    HALVES = [(h, slice(128 * h, 128 * h + 128)) for h in range(2)]

    def codes(t):
        for h, c in HALVES:
            tt(T.pd[:, c], T.bA[:, c], T.xx[:, c], A.mult, "bA xx", "pd%d" % h)
        for h, c in HALVES:
            ts(T.z[:, c], T.pd[:, c], col(KC + t), 2.0 ** 30, A.add, A.min, "pd%d fk%d" % (h, t), "z%d" % h)
        for h, c in HALVES:
            ts(T.ci[:, c], T.z[:, c], 4, 8191 | 0x7FFF8000, A.arith_shift_right, A.bitwise_and, "z%d" % h, "ci%d" % h)

    def offsets():
        for h, c in HALVES:
            ts(T.off[:, c], T.ci[:, c], float(VOID), None, A.min, None, "ci%d" % h, "off+")

    codes_start()
    m128 = T.mf[:, 0:128]
    ts(T.segm[:], T.mif[:], 0.0, None, A.is_gt, None, "mif", "segm")
    ts(col(KC), col(PI), 16.0 * 613, None, A.mult, None, "f0", "fk0")
    ts(T.I1[:], m128, col(PP), None, A.is_equal, None, "mf f2", "I1")
    ts(T.If[:], m128, col(PP), None, A.is_equal, None, "mf f2", "If")
    ts(T.nIf[:], m128, col(PP), -1.0, A.is_equal, A.mult, "mf f2", "nIf")
    act(T.BLKN[:], T.BLK[:], F.Copy, "BLK", "BLKN", scale=NONE)
    for k in range(2):
        act(T.D0C[:, 256 * k:256 * k + 256], T.segm[:], F.Identity, "segm", "D0C+", scale=2.0 ** 20 + 1, bias=-2.0 ** 20)
    act(T.s0[:], T.q1[:], F.Copy, "q1", "s0", scale=16384.0)
    act(T.q2[:], T.q1[:], F.Square, "q1", "q2", bias=8.0)
    act(T.s2[:], T.q1[:], F.Copy, "q1", "s2", scale=-512.0)
    act(T.s1[:], T.q2[:], F.Identity, "q2", "s1", scale=-8192.0, bias=8192.0 * 65)
    ts(T.pd[:], T.tsti[:], 256.0, NONE, A.is_ge, A.mult, "tsti", "pd0 pd1")
    tt(T.T0[:], T.pd[:], T.tsti[:], A.max, "pd0 pd1 tsti", "T0")
    codes_y(0)
    codes_x(0)
    act(T.s3[:], T.q2[:], F.Identity, "q2", "s3", scale=256.0, bias=-16384.0)
    act(T.dm[:], T.mf[:], F.Copy, "mf", "dm", scale=1.0 / 1024)
    act(T.I256[:], T.I1[:], F.Copy, "I1", "I256", scale=256.0)
    act(T.nI[:], T.I1[:], F.Copy, "I1", "nI", scale=-4096.0)
    codes(0)
    offsets()
    for i in range(16):
        if i < 6:
            act(T.PX[:, i:4096:16], T.prb[:], F.Copy, "prb", "PXs+")
        else:
            cp(T.PX[:, i:4096:16], T.prb[:], "prb", "PXv+")
    act(T.nI16[:], T.I1[:], F.Copy, "I1", "nI16", scale=-16.0)
    act(T.D0G[:], T.segm[:, 0:128], F.Identity, "segm", "D0G", scale=2.0 ** 25 + 16, bias=-2.0 ** 25)
    act(T.D0V[:], T.segm[:, 0:128], F.Identity, "segm", "D0V", scale=2.0 ** 27 + 256, bias=-2.0 ** 27)
    ms(T.U[:, W:VOID], 0.0, "Uc+")
    ms(T.U[:, VOID:UW], -128.0, "Uc+")
    cp(T.prb2[:, 0:128 - NS], T.prb[:, 128:256 - NS], "prb", "prb2+")
    ms(T.prb2[:, 128 - NS:128], 0.0, "prb2+")
    ts(T.Ind[:], T.w8[:], col(PG), 256.0, A.is_equal, A.mult, "w8 f1", "Ind")
    for h in range(2):
        ts(T.TH0[:, h, :], T.thb[:], 256.0, -SQ, A.mult, A.add, "thb", "TH0+")
    act(T.TH20[:], T.TH0[:], F.Identity, "TH0", "TH20", bias=SQ)
    ts(col(RC_), col(PI), float(RHO[0]), NONE, A.is_equal, A.mult, "f0", "fr0")
    ms(T.FE[:, :, 48:56], 1.0, "F6")
    ms(T.FE2[:, :, 40:48], 1.0, "E5")

    def fills(n, rows, items):
        for f, v in items:
            sel(T[n][0:rows, :], T[n][0:rows, :], BP, A.not_equal, v, -8 * f, 1, n, n)

    def tn(t):
        sel(T.TN[:, 128 * t:128 * t + 128], T.TNb[:], [[0, 8], [1, 16]], A.not_equal, 0.0, -RHO[t], 0, "TNb", "TN%d" % t)

    def ct(t):
        n, a = "CT%d" % t, 128 * t
        sel(T.CT[0:K2R, a:a + 128], T.CTa[0:K2R, :], [[0, 8], [1, 16]], A.not_equal, 0.0, -RHO[t], 0, "CTa", n)
        c = T.CT[0:K2R, a + RHO[t]:a + 128:16]
        for f, v in ((0, -16.0), (1, 1.0), (2, NONE), (5, 240.0)):
            sel(c, c, [[-1, 8]], A.not_equal, v, -8 * f, 1, n, n)

    sel(T.s0[0:K1R, :], T.s0[0:K1R, :], BP, A.is_equal, 0.0, 0, 1, "s0", "s0")
    sel(T.s1[0:K1R, :], T.s1[0:K1R, :], BP, A.is_equal, 0.0, -8 * 6, 1, "s1", "s1")
    sel(T.s2[0:K1R, :], T.s2[0:K1R, :], BP, A.is_equal, 0.0, -8, 1, "s2", "s2")
    sel(T.s3[0:K1R, :], T.s3[0:K1R, :], BP, A.is_equal, 0.0, -8 * 6, 1, "s3", "s3")
    fills("s0", K1R, [(2, -8192.0)])
    fills("s2", K1R, [(3, 256.0)])
    fills("CTa", K2R, [(4, 1.0)])
    fills("s0", K1R, [(4, -8192.0)])
    fills("CTa", K2R, [(2, -NONE)])
    fills("CC", K1R, [(2, 2.0 ** 17)])
    fills("CTa", K2R, [(3, NONE)])
    fills("CC", K1R, [(0, 2.0 ** 17)])
    fills("CTa", K2R, [(5, 2 * NONE)])
    fills("CC", K1R, [(4, 2.0 ** 17)])
    sel(T.TNb[:], T.BLKN[:], [[1, 128]], A.is_gt, 0.0, 0, -1, "BLKN", "TNb")
    sel(T.TNb[:], T.TNb[:], [[1, 128]], A.not_equal, -NONE, 0, -1, "TNb", "TNb")
    tn(0)
    fills("CC", K1R, [(5, 1.0)])
    ct(0)
    fills("CC", K1R, [(6, 201.0 * 8192)])

    def late_columns():
        ms(T.half[:], 0.5, "half")
        ms(T.pw2[:], 0.0, "pw2")
        ts(col(R14), col(PI), 14.0, None, A.is_equal, None, "f0", "f10")
        ts(col(R15), col(PI), 15.0, None, A.is_equal, None, "f0", "f11")
        ts(col(HB), col(PI), 14.0, 0.5, A.is_lt, A.mult, "f0", "f12")
        scan(T.pw[:], T.half[:], T.pw2[:], A.mult, A.add, "half pw2", "pw", 2.0)
        tt(col(CL), col(HB), col(R14), A.subtract, "f12 f10", "f7")
        tt(col(CR), col(HB), col(R15), A.subtract, "f12 f11", "f8")
        ts(T.pw2[:], T.mif[:, 0:16], col(PI), None, A.is_equal, None, "mif f0", "pw2")
        ts(col(N14), col(R14), -1.0, None, A.mult, None, "f10", "f9")
        tt(T.pw[:], T.pw[:], T.pw2[:], A.mult, "pw pw2", "pw")
        op("v", lambda: V.tensor_reduce(col(SK), T.pw[:, 0:14], AxisListType.X, A.add), "pw", "f5")
        ts(T.bH[:, 0:256], T.dm[:], col(R15), col(CL), A.mult, A.add, "dm f11 f7", "bH")
        ts(T.bH[:, 256:512], T.dm[:], col(N14), col(CR), A.mult, A.add, "dm f9 f8", "bH")
        ts(col(BK), col(SK), 0.5, -0.5, A.mult, A.add, "f5", "f6")

    def late_tiles():
        for k in range(1, 4):
            ts(col(KC + k), col(PI), 16.0 * 613, 16.0 * 77 * k, A.mult, A.add, "f0", "fk%d" % k)
            ts(col(RC_ + k), col(PI), float(RHO[k]), NONE, A.is_equal, A.mult, "f0", "fr%d" % k)
        ts(T.MQ[:], T.mif[:], col(PI), None, A.is_equal, None, "mif f0", "MQ")
        ts(T.TM[:], T.mf[:], float(TR), None, A.add, None, "mf", "TM")
        ms(T.SEL[:, 0:112], 0.0, "SEL+")
        ms(T.SEL[:, 128:240], 0.0, "SEL+")
        ms(T.SEL[:, 112:128], 2.0 ** 24, "SEL+")
        tt(T.TM[:], T.TM[:], T.MQ[:], A.mult, "TM MQ", "TM")

    late_columns()

    def fe(f, n=1):
        return T.FE[:, :, 8 * f:8 * (f + n)]

    def fe2(f, n=1):
        return T.FE2[:, :, 8 * f:8 * (f + n)]

    ALLF = " ".join("F%d" % k for k in range(7)) + " I1"
    ALLE = " ".join("E%d" % k for k in range(6)) + " I1"
    GB, VB = [T.bA, T.bB], [T.bC, T.bD]
    GN, VN = ["bA", "bB"], ["bC", "bD"]
    win = T.U[:, 0:UW]
    FT, FT2 = T.FT[0:K1R, :], T.FT2[0:K2R, :]
    X0 = 4096 - 16 * NS

    def gains(h, t):
        a, b = 2048 * h, 2048 * h + 2048
        mm(GB[h][:, 0:128], T.prb[:, 0:128] if h == 0 else T.prb2[:], T.nI[:], True, False, ("prb" if h == 0 else "prb2") + " nI", GN[h])
        for i in range(16):
            mm(GB[h][:, 0:128], T.Mx[:, a + i:b:16], T.I256[:], False, False, ("Mx0" if h == 0 else "Mx1 Mx2") + " I256", GN[h])

    def votes(h):
        a, b = 2048 * h, 2048 * h + 2048
        mm(VB[h][:, 0:128], T.hib[:, 128 * h:128 * h + 128], T.If[:], True, False, "hib If", VN[h])
        for i in range(16):
            mm(VB[h][:, i:128:16], T.got[:, a + i:b:16], T.Ind[:], False, i == 15, ("got0" if h == 0 else "got1 got2") + " Ind", VN[h])

    for t in range(4):
        src = "T%d" % t
        for k, a, b in ((2, X0, 4096), (0, 0, 2048), (1, 2048, X0)):
            act(T.got[:, a:b], win.indirect(T.off[:, a // 16:b // 16]), F.Identity, "off " + UALL, "got%d" % k, scale=16.0, bias=-2048.0)
            if k == 0:
                mm(T.bG[:], T.nI16[:], T.PX[:, X0:4096], True, False, "nI16 PXs PXv", "bG")
                mm(T.bG[:], T.I1[:], T.got[:, X0:4096], False, True, "I1 got2", "bG")
                act(T.Mx[:, X0:4096], T.bG[:], F.Relu, "bG", "Mx2", scale=1.0 / 16, bias=128.0)
        op("v", lambda: V.tensor_tensor(T.Mx[:, 0:2048], win.indirect(T.off[:, 0:128]), T.PX[:, 0:2048], A.max),
           "off PXs PXv " + UALL, "Mx0")
        ts(T.hib[:], T.off[:], 1.0 / 32, 1024.0 - 0.484375, A.mult, A.add, "off", "hib")
        op("v", lambda: V.tensor_tensor(T.Mx[:, 2048:X0], win.indirect(T.off[:, 128:256 - NS]), T.PX[:, 2048:X0], A.max),
           "off PXs PXv " + UALL, "Mx1")
        gains(0, t)
        votes(0)
        gains(1, t)
        votes(1)
        act(T.Nn[:], T[src][:], F.Relu, src, "Nn", bias=1.0 - NONE)
        act(T.Tt[:], T[src][:], F.Identity, src + " fr%d" % t, "Tt", bias=col(RC_ + t))
        def payload(h):
            c = slice(2048 * h + 15, 2048 * h + 2048, 16)
            ts(T.R[:, 128 * h:128 * h + 128], T.K1[:, c], SQ - 7.5, SQ - 2288.0, A.add, A.max, "K1%d" % h, "R%d" % h)
            mm(GB[h][:, 0:128], T.K1[:, c], T.If[:], False, False, "K1%d If" % h, GN[h])
            mm(GB[h][:, 0:128], T.R[:, 128 * h:128 * h + 128], T.nIf[:], False, True, "R%d nIf" % h, GN[h])

        def best(h):
            scan(T.GKs[:, h, :], T.D0G[:], GB[h][:, 0:128], A.add, A.max, "D0G " + GN[h], "GKs+")

        for h in (0, 1, 2, 3, 7, 4, 5, 6):
            a, b = 512 * h, 512 * h + 512
            scan(T.K1[:, a:b], T.D0C[:], T.got[:, a:b], A.add, A.max, "D0C got%d" % (2 if h == 7 else h // 4), "K1%d+" % (h // 4))
            if h == 7:
                payload(0)
        best(0)
        payload(1)
        mm(T.bF[:, 0:256], T.TN[:, 128 * t:128 * t + 128], T.Nn[:], True, False, "TN%d Nn" % t, "bF")
        best(1)
        gk = T.GKs[:, :, 15:128:16]
        th, thn = (T.TH0, "TH0") if t == 0 else (T.TH, "TH")
        th2, thn2 = (T.TH20, "TH20") if t == 0 else (T.TH2, "TH2")
        ts(T.GKi[:], gk, SQ, 240.0, A.add, A.max, "GKs", "GKi")
        tt(fe(4), gk, th[:], A.is_lt, "GKs " + thn, "F4")
        ts(T.DEC[:, :, 0:8], T.GKi[:], 15, None, A.bitwise_and, None, "GKi", "DEC0")
        ts(T.DEC[:, :, 8:16], T.GKi[:], 4, 15, A.arith_shift_right, A.bitwise_and, "GKi", "DEC1")
        cp(fe(0, 2), T.DEC[:, :, 0:16], "DEC0 DEC1", "F0 F1")
        act(T.FE[:, 0, 40:48], T.FE[:, 0, 32:40], F.Copy, "F4 f2", "F5+", scale=col(PP))
        act(T.FE[:, 1, 40:48], T.FE[:, 1, 32:40], F.Copy, "F4 f13", "F5+", scale=col(PH))
        act(fe(2, 2), fe(0, 2), F.Square, "F0 F1", "F2 F3", bias=-8.0)
        mm(T.bE[0:K1R, 0:128], T.FE[:, 0, :], T.I1[:], True, True, ALLF, "bE")
        mm(T.bB[0:K1R, 0:128], T.FE[:, 1, :], T.I1[:], True, True, ALLF, "bB")
        act(T.FT[0:K1R, 0:128], T.bE[0:K1R, 0:128], F.Copy, "bE", "FTa")
        for h in range(2):
            scan(T.VKs[:, h, :], T.D0V[:], VB[h][:, 0:128], A.add, A.max, "D0V " + VN[h], "VKs+")
        vk = T.VKs[:, :, 15:128:16]
        cp(T.FT[0:K1R, 128:256], T.bB[0:K1R, 0:128], "bB", "FTb")
        if t == 0:
            tt(T.CP[0:K1R, :], T.s0[0:K1R, :], T.s1[0:K1R, :], A.add, "s0 s1", "CP")
            tt(T.CX[0:K1R, :], T.s2[0:K1R, :], T.s3[0:K1R, :], A.add, "s2 s3", "CX")
        tt(fe2(2), T.GKi[:], th2[:], A.is_lt, "GKi " + thn2, "E2")
        ts(fe2(3), vk, -2.0 ** 23, None, A.is_lt, None, "VKs", "E3")
        ts(T.VKi[:], vk, 2.0 ** 23 - 1024, None, A.add, None, "VKs", "VKi")
        ts(T.DEC[:, :, 16:24], T.GKi[:], 8, 15, A.arith_shift_right, A.bitwise_and, "GKi", "DEC2")
        ts(T.tki[:], T.VKi[:], 255, None, A.bitwise_and, None, "VKi", "tki")
        cp(fe2(0, 2), T.DEC[:, :, 8:24], "DEC1 DEC2", "E0 E1")
        cp(fe2(4), T.tki[:], "tki", "E4")
        mm(T.bA[:, 0:256], T.CP[0:K1R, :], FT, True, True, "CP FTa FTb", "bA")
        colA = [(T.bG[:, 256:384], "bG"), (T.bD[:, 0:128], "bD")]
        for h, c in HALVES:
            mm(colA[h][0], T.CC[0:K1R, :], T.FT[0:K1R, c], True, False, "CC FT" + "ab"[h], colA[h][1])
        for h in range(2):
            mm(T.bC[0:K2R, 128 * h:128 * h + 128], T.FE2[:, h, :], T.I1[:], True, True, ALLE, "bC")
        if t < 3:
            for h in range(2):
                mm(T.bC[:, 256 + 8 * h:264 + 8 * h], T.onesb[:, 0:128], T.FE2[:, h, 16:24], True, True, "onesb E2", "bC")
        act(FT2, T.bC[0:K2R, 0:256], F.Copy, "bC", "FT2")
        for h, c in HALVES:
            tt(T.Z[:, c], T.bA[:, c], T.ci[:, c], A.min, "bA ci%d" % h, "Z%d" % h)
            mm(colA[h][0], T.BLK[:], T.Z[:, c], False, True, "BLK Z%d" % h, colA[h][1])
        mm(T.bF[:, 0:256], T.CT[0:K2R, 128 * t:128 * t + 128], FT2, False, True, "CT%d FT2" % t, "bF")
        mm(T.bE[:, 256:512], T.CX[0:K1R, :], FT, True, True, "CX FTa FTb", "bE")
        for h, c in HALVES:
            ts(T.A1[:, c], colA[h][0], col(SK), col(BK), A.mult, A.add, colA[h][1] + " f5 f6", "A1%d" % h)
        mm(T.bG[:, 0:256], T.CC[0:K1R, :], FT, True, False, "CC FTa FTb", "bG")
        mm(T.bG[:, 0:256], T.BLK[:], T.Z[:], False, False, "BLK Z0 Z1", "bG")
        tt(T["Tn%d" % t][:], T.bF[:, 0:256], T.Tt[:], A.min, "bF Tt", "Tn%d" % t)
        if t < 3:
            act(T.junk[:], T.bC[:, 256:272], F.Copy, "bC", "junk msum", accum_out=T.msum[:, 0:1])
        act(T.Xs[:], T.bE[:, 256:512], F.Copy, "bE", "Xs")
        dst = T.cores[(rank + 1) % N] if t < 3 else T.cores[(rank - 3) % N]
        es = topo.engines(core, dst)[::2]
        need("g", deps_of("g", ["Tn%d" % t], []))
        rid, pid, _s = topo.addr(dst)
        g.remote_dma(T["T%d" % (t + 1)][:], T["Tn%d" % t][:], T.sem["a%d" % (t + 1)], T.sem.loc, pid, rid, sum(1 << e for e in es))
        wr["T%d" % (t + 1)] = ("a%d" % (t + 1), len(es))
        nloc = len(es)
        if t < 3:
            rot(t + 1)
            tn(t + 1)
            ct(t + 1)
        for h, c in HALVES:
            ts(T.A2[:, c], T.A1[:, c], 1, None, A.bitwise_and, None, "A1%d" % h, "A2%d" % h)
        for h, c in HALVES:
            tt(T.lhs[:, c], T.A2[:, c], T.bH[:, c], A.subtract, "A2%d bH" % h, "lhs+")
        tt(T.rhs[:], T.A2[:], T.bH[:, 256:512], A.subtract, "A20 A21 bH", "rhs")
        ts(T.lhsO[:], T.lhs[:], col(OD), None, A.mult, None, "lhs f3", "lhsO")

        def gram(bn, pos, gr, half):
            ba = 32 * (gr // 2)
            l, ln, k = (T.lhs, "lhs", 16) if gr % 2 == 0 else (T.lhsO, "lhsO", 32)
            n, c0 = (256, 0) if half == 0 else (128, 128)
            mm(T[bn][:, pos:pos + n], l[ba:ba + k, c0:c0 + 128], T.rhs[ba:ba + k, c0:256], True, True, ln + " rhs", bn)

        for gr in (0, 2, 1, 3, 4, 5, 6, 7):
            gram("b" + "ABCD"[gr // 2], 256 * (gr % 2), gr, 0)
        last = {}
        for bn, pair in (("bE", 0), ("bF", 2), ("bE", 1), ("bF", 3)):
            if bn in last:
                need("t", [("t", last[bn])])
            for k in range(2):
                gram(bn, 256 * (pair % 2) + 128 * k, 2 * pair + k, 1)
            last[bn] = cnt["t"]
        if t == 0:
            late_tiles()
        for k, bn, q in ((0, "bA", "v"), (1, "bB", "s"), (2, "bC", "v"), (3, "bD", "s"), (4, "bE", "v"), (5, "bF", "s")):
            mt = T["mt%d" % k]
            if k == 5 and t < 3:
                codes_x(t + 1)
            if q == "s":
                act(mt[:], T[bn][:], F.Relu, bn, "mt%d" % k, bias=-3.5)
            else:
                ts(mt[:], T[bn][:], -3.5, 0.0, A.add, A.max, bn, "mt%d" % k)
        for gr in range(8):
            if gr == 4 and t < 3:
                codes_start()
                codes_y(t + 1)
            mm(T.bG[:, 0:256], T.SEL[:, 112 - 16 * gr:240 - 16 * gr], T["mt%d" % (gr // 2)][:, 256 * (gr % 2):256 * (gr % 2) + 256],
               False, False, "SEL mt%d" % (gr // 2), "bG")
        for gr in range(8):
            mm(T.bG[:, 128:256], T.SEL[:, 112 - 16 * gr:240 - 16 * gr], T["mt%d" % (4 + gr // 4)][:, 128 * (gr % 4):128 * (gr % 4) + 128],
               False, gr == 7, "SEL mt%d" % (4 + gr // 4), "bG")
        if t < 3:
            codes(t + 1)
            act(T.m16[:, 0:1], T.msum[:, 0:1], F.Identity, "msum", "m16", bias=49152.0 - 127.5)
            act(T.msum[:, 1:2], T.msum[:, 0:1], F.Identity, "msum", "mb", scale=256.0, bias=256.0 * 49152)
            act(T.msum[:, 2:3], T.m16[:, 0:1], F.Identity, "m16 mb", "mc", scale=-256.0, bias=T.msum[:, 1:2])
            act(T.TH[:], T.TH0[:], F.Identity, "TH0 mc", "TH", bias=T.msum[:, 2:3])
            act(T.TH2[:], T.TH20[:], F.Identity, "TH20 mc", "TH2", bias=T.msum[:, 2:3])
        for h, c in HALVES:
            tt(T.dm[:, c], T.bG[:, c], T.TM[:, c], A.min, "bG TM", "dm%d" % h)
        if t < 3:
            offsets()
        for h, c in HALVES:
            scan(T.D1[:, c], T.segm[:, c], T.dm[:, c], A.mult, A.add, "segm dm%d" % h, "D1%d" % h)
        for h in range(2):
            cp(T.l2u[:, 8 * h:8 * h + 8], T.D1[:, 128 * h + 15:128 * h + 128:16], "D1%d" % h, "l2u+")
        op("v", lambda: V.tensor_tensor(T.vals[:], win.indirect(T.l2u[:]), T.Xs[:], A.min), "l2u Xs " + UALL, "vals")
        op("v", lambda: V.tensor_copy(win.indirect(T.l2u[:]), T.vals[:]), "l2u vals", UALL)

    for k in range(16):
        mm(T.bA[:, 0:384], T.I1[:], T.U[:, k:6144:16], k == 0, k == 15, "I1 " + UALL, "bA")
    for k in range(8):
        scan(T.ysc[:, 256 * k:256 * k + 256], T.segm[:], T.U[:, 6144 + 256 * k:6400 + 256 * k], A.mult, A.add, "segm " + UALL, "ysc+")
    cp(T.yc32[:, 384:512], T.ysc[:, 15:2048:16], "ysc", "yc1")
    ts(T.yt32[:], T.T4[:], 256.0, None, A.min, None, "T4", "yt32")
    act(T.yc32[:, 0:384], T.bA[:, 0:384], F.Copy, "bA", "yc0")
    dma("s", T.yt[:], T.yt32[:], "yt32", "yt")
    dma("y", T.yc[:], T.yc32[:], "yc0 yc1", "yc")
    fin = [(q, n) for q, n in cnt.items() if n] + [("d%d" % k, 16) for k in range(ndma[0])]
    need("g", fin)
    g.wait_ge(T.sem.loc, 4 * nloc)
